import numpy as np, ml_dtypes
CORES = [25,29,65,69,153,157,193,197]
N = 8
BF = ml_dtypes.bfloat16
V, L, D, M, Q, RO = 4096, 192, 5, 16, 4, 3
def partners(rng):
    nt = np.zeros((8, 16, D), np.int64)
    for g in range(8):
        for e in range(D):
            o = rng.permutation(16); nt[g, o[::2], e] = o[1::2]; nt[g, o[1::2], e] = o[::2]
    return nt
def pairwise(nt, a):
    rep = np.minimum(np.arange(16)[:, None], nt[:, :, 0:1])
    return np.take_along_axis(a, np.broadcast_to(rep, a.shape), 2)
def parts(rng):
    mu = rng.integers(-160, 161, (N, 8, 1, V)) * rng.integers(0, 2, (N, 8, 1, V))
    x = np.clip(rng.integers(-256, 256, (N, 8, 16, V)) + mu, -256, 255)
    nt = partners(rng); w = rng.integers(0, V, (N, 8, 16, L)); z = rng.integers(-256, 256, (N, 8, 16, L))
    kind = rng.random((N, 8, 1, L)); free = rng.integers(0, D + 1, (N, 8, 16, L)); low = pairwise(nt, rng.integers(0, 2, (N, 8, 16, L)))
    d = np.where(kind < 0.5, 0, np.where(kind < 0.8, low, np.where(kind < 0.98, free, D)))
    return x, nt, w, d, z
def pack(x, nt, w, d, z):
    return {"xs": np.ascontiguousarray(x.reshape(N, 128, V)).astype(np.float32).astype(BF), "nt": np.ascontiguousarray(np.broadcast_to(nt.reshape(1, 128, D), (N, 128, D))).astype(np.int32),
            "w0": np.ascontiguousarray(w.reshape(N, 128, L)).astype(np.int32), "d0": np.ascontiguousarray(d.reshape(N, 128, L)).astype(np.int32),
            "z0": np.ascontiguousarray(z.reshape(N, 128, L)).astype(np.float32).astype(BF)}
def setup_inputs(rng):
    return pack(*parts(rng))
def setup_inputs_corners(rng):
    x, nt, w, d, z = parts(rng); ar = np.arange(16)
    kind = rng.integers(0, 8, (N, 8, 1, L))
    for q in range(N):
        kind[q, q % 8] = 0; kind[q, (q + 1) % 8] = 1
    k0 = rng.integers(0, 16, 8)[:, None]
    p0 = ((ar == k0) | (nt[:, :, 0] == k0))[:, :, None]; p1 = ((ar == k0) | (nt[:, :, D - 1] == k0))[:, :, None]; low = ar[:, None] < nt[:, :, 0:1]
    two = (D - 1) * pairwise(nt, rng.integers(0, 2, (N, 8, 16, L))); d = rng.integers(0, D + 1, (N, 8, 16, L))
    for c, v in ((0, D), (1, D - 1), (2, np.where(p0, 0, D)), (3, np.where(low, 0, D)), (4, 0), (5, two), (7, np.where(p1, D - 1, D))):
        d = np.where(kind == c, v, d)
    kn = rng.integers(0, 4, (N, 8, 1, L)); near = np.where((np.arange(L) & 1) == 1, rng.integers(V - 32, V, (N, 8, 16, L)), w[:, :, :1])
    w = np.where(kn == 0, 0, np.where(kn == 1, V - 1, np.where(kn == 2, near, w)))
    z = np.where(rng.random(z.shape) < 0.5, z, np.where(rng.random(z.shape) < 0.5, -256, 255))
    return pack(x, nt, w, d, z)
def setup_inputs_crowd(rng):
    x, nt, w, d, z = parts(rng); o = int(rng.integers(0, 8))
    for g in range(8):
        ty = (g + o) % 8; k0 = int(rng.integers(0, 16)); l0 = int(nt[g, k0, 0])
        if ty in (0, 1): w[:, g] = rng.integers(0, V, (N, 1, 1))
        if ty == 1:
            w[:, g, k0] = rng.integers(0, V, (N, L)); w[:, g, l0] = rng.integers(0, V, (N, L))
        if ty == 2:
            x[:, g] = 0
            for r in range(1, N):
                lo, hi = ((189, 195), (-194, -186))[((r - 1) // 2) % 2]
                x[r, g] = rng.integers(lo, hi, (16, V))
        if ty == 3: x[:, g] = (np.argsort(rng.random((N, 16, V)), axis=1) < rng.integers(7, 10, (N, 1, V))).astype(np.int64)
        if ty in (4, 5): x[:, g] = np.where(rng.random((N, 1, V)) < 0.5, -256, 255)
        if ty == 4:
            off = (np.arange(16)[:, None] == rng.integers(0, 16, (N, 1, V))) & (rng.random((N, 1, V)) < 0.5)
            x[:, g] = np.where(off, np.where(x[:, g] < 0, -255, 254), x[:, g])
        if ty == 5: x[:, g, int(rng.integers(0, 16))] = 0
        if ty in (6, 7): w[:, g] = rng.choice(np.array([0, V - 1, 5]), (N, 16, L))
        if ty == 6:
            x[:, g] = np.where(rng.random((N, 16, V)) < 0.05, x[:, g], rng.integers(-6, 7, (N, 16, V)))
            ar = np.arange(16); lead = np.minimum(ar, nt[g, :, 0]); some = rng.permutation(ar[lead == ar])[:4]
            side = np.any(lead[:, None] == some[None, :], axis=1).astype(np.int64); up = (lead == ar).astype(np.int64)
            four = rng.integers(0, V, (N, 4, L)); w[:, g] = np.where(rng.random((N, 1, L)) < 0.5, four[:, 2 * side + up], w[:, g])
        if ty != 7: d[:, g] = 0
    return pack(x, nt, w, d, z)
def setup_inputs_ends(rng):
    nt = partners(rng)
    for g in range(8):
        for e in range(D):
            o = 1 + rng.permutation(14); nt[g, 0, e] = 15; nt[g, 15, e] = 0; nt[g, o[::2], e] = o[1::2]; nt[g, o[1::2], e] = o[::2]
            if (g + e) % 2 == 0: nt[g, :, e] = 15 - np.arange(16)
    x = np.where(rng.random((N, 8, 16, V)) < rng.choice(np.array([0.0, 0.25, 0.5, 0.75, 1.0]), (N, 8, 1, V)), 255, -256)
    hp = (((V - 1) ** 2 >> 5) + 2 * (V - 1)) & (V - 1)
    for q in range(N):
        for g in range(8):
            kd = (7 - g + N - 1 - q) % 4
            for e in range(D):
                o = [rng.permutation(16) for _ in range(3)]
                if kd == 0: on = (o[0], o[1][:0], o[2][:0])
                elif kd == 1: on = (o[0][:8], o[0][8:], o[2])
                elif kd == 2: on = (o[0][:7], o[1][:8], o[2][:9])
                else: on = (o[0][:15], o[1][:15], o[2][:15])
                for c, rows in zip((0, V - 1, hp), on):
                    col = np.full(16, -256, np.int64); col[rows] = 255; x[q, g, :, (c + 77 * e) & (V - 1)] = col
    w = (V - 1) * rng.integers(0, 2, (N, 8, 16, L)); z = np.where(rng.random((N, 8, 16, L)) < 0.5, -256, 255)
    d = D * pairwise(nt, (rng.random((N, 8, 16, L)) < 0.2).astype(np.int64))
    d = np.where(rng.random((N, 8, 1, L)) < 0.1, D * rng.integers(0, 2, (N, 8, 16, L)), d)
    for g in range(8):
        own = np.nonzero(np.arange(16) < nt[g, :, 0])[0]
        for i in (0, L - 1):
            d[:, g, :, i] = 0
            for j in range(8):
                k = int(own[j]); w[:, g, k, i] = (0, 0, V - 1)[j % 3]; w[:, g, int(nt[g, k, 0]), i] = (0, V - 1, V - 1)[j % 3]
    return pack(x, nt, w, d, z)
def setup_inputs_spread(rng):
    x, nt, w, d, z = parts(rng)
    x = (np.exp2(8 * rng.random((N, 8, 1, V))) * (2 * rng.random((N, 8, 16, V)) - 1)).astype(np.int64)
    x = np.where(rng.random((N, 8, 1, V)) < 0.0625, 0, x)
    w = np.minimum((np.exp2(12 * rng.random((N, 8, 16, L))) - 1).astype(np.int64), V - 1)
    z = (np.exp2(8 * rng.random((N, 8, 1, L))) * (2 * rng.random((N, 8, 16, L)) - 1)).astype(np.int64)
    return pack(x, nt, w, d, z)
def setup_inputs_ties(rng):
    x, nt, w, d, z = parts(rng)
    base = rng.integers(-256, 256, (N, 8, 16)); few = np.where(rng.random((N, 8, 16)) < 0.5, -3, 4); few[:, :, 0] = -3; few[:, :, 1] = 4; base[:, ::2] = few[:, ::2]
    ix = ((2 * rng.integers(0, 8, (N, 8, 1, V)) + 1) * np.arange(16)[:, None] + rng.integers(0, 16, (N, 8, 1, V))) & 15
    x = np.take_along_axis(np.ascontiguousarray(np.broadcast_to(base[..., None], (N, 8, 16, V))), ix, 2)
    w = np.where(rng.random((N, 8, 1, L)) < 0.3, rng.choice(np.array([0, 1, 64, V - 1]), (N, 8, 16, L)), w)
    return pack(x, nt, w, d, z)
def check_inputs(d):
    bad = []
    for k, lo, hi in (("xs", -256, 255), ("nt", 0, 15), ("w0", 0, V - 1), ("d0", 0, D), ("z0", -256, 255)):
        a = np.asarray(d[k]).astype(np.float64)
        if not (np.min(a) >= lo and np.max(a) <= hi): bad.append("range of " + k)
        elif np.any(a != np.floor(a)): bad.append("whole numbers of " + k)
    nt = np.asarray(d["nt"])
    if "range of nt" not in bad:
        a = nt.astype(np.int64).reshape(N, 8, 16, D); own = np.arange(16).reshape(16, 1)
        if np.any(np.take_along_axis(a, a, 2) != own) or np.any(a == own): bad.append("pairs of nt")
    if np.any(nt != nt[:1]): bad.append("nt alike on all ranks")
    return bad
def reference(xs, nt, w0, d0, z0):
    X = xs.astype(np.float32).astype(np.int32).reshape(N, 8, 16, V); W = w0.astype(np.int64).reshape(N, 8, 16, L); dep = d0.astype(np.int64).reshape(N, 8, 16, L)
    z = z0.astype(np.float32).astype(np.int32).reshape(N, 8, 16, L); tab = nt[0].astype(np.int64).reshape(8, 16, D); A = np.zeros((N, 8, L), np.int64)
    kk = np.arange(16).reshape(1, 16, 1); mm = np.arange(M).reshape(1, M, 1); lanes = np.arange(L).reshape(1, L)
    for t in range(RO):
        Xn = np.array(X)
        for r in range(N):
            p = (r + t) % N; q = (p + 1) % N; w = W[r]; d = dep[r]
            l = np.take_along_axis(tab, np.minimum(d, D - 1), 2); wl = np.take_along_axis(w, l, 1); dl = np.take_along_axis(d, l, 1)
            act = (d < D) & (dl == d)
            ix = (((w * wl) >> 5) + w + wl + 77 * d) & (V - 1)
            b = np.take_along_axis(X[p], ix.reshape(8, 1, 16 * L), 2).reshape(8, 16, 16, L)
            s = np.add.reduce(b, axis=1, dtype=np.int64)
            wt = np.where(act, np.left_shift(1, D - d), 0)
            sg = np.sign(s[:, None, :, :] - s[:, :, None, :])
            score = np.abs(np.add.reduce(wt[:, None, :, :] * sg, axis=2)); score = np.where(act, score, 2 ** 20)
            e = np.argmin(score, axis=1); live = np.any(act, axis=1)
            lam = np.take_along_axis(b, e[:, None, None, :], 2)[:, :, 0]
            u = np.add.reduce((2 * kk + 1) * lam, axis=1, dtype=np.int64); v = np.add.reduce(lam, axis=1, dtype=np.int64)
            hx = ((2 * mm + 1) * u[:, None, :] + mm * v[:, None, :] + 333 * mm) & (V - 1)
            c = np.take_along_axis(X[q], hx.reshape(8, 1, M * L), 2).reshape(8, 16, M, L)
            f = (np.max(c, axis=2) + np.min(c, axis=2)) >> 1
            up = np.add.reduce(f > lam, axis=1, dtype=np.int64) >= 8 + (A[r] & 1)
            le = np.add.reduce(b <= lam[:, :, None, :], axis=1, dtype=np.int64); ge = np.add.reduce(b >= lam[:, :, None, :], axis=1, dtype=np.int64)
            hit = act & ((np.where(up[:, None, :], le, ge) >= 9) | (kk == e[:, None, :]) | (l == e[:, None, :]))
            W[r] = np.where(hit & (up[:, None, :] == ((s & 1) == 1)), wl, w); dep[r] = d + hit
            A[r] = np.add.reduce(hit, axis=1, dtype=np.int64) >> 1
            slot = np.broadcast_to((Q * lanes + (u & (Q - 1)))[:, None, :], (8, 16, L))
            np.put_along_axis(Xn[p], slot, np.where(live[:, None, :], (lam + z[r]) >> 1, np.take_along_axis(X[p], slot, 2)), 2)
            z[r] = np.where(live[:, None, :], lam, z[r])
        X = Xn
    return {"wn": W.reshape(N, 128, L).astype(np.float32), "dn": dep.reshape(N, 128, L).astype(np.float32), "zn": z.reshape(N, 128, L).astype(np.float32).astype(BF),
            "xn": np.ascontiguousarray(X.reshape(N, 128, V)[:, :, :L * Q]).astype(np.float32).astype(BF)}

@@ -1,0 +1,691 @@
+import math
+import numpy as np
+from concourse.bass import DstId, RemoteDMATransfer
+from concourse.mybir import AluOpType as ALU
+from concourse.mybir import ActivationFunctionType as ACT
+
+V, L, D, RO, NR = 4096, 192, 5, 3, 8
+NCH = 3
+n = L // NCH
+C = n // 16
+SL, SG = 5, 8
+WR = 4 * L
+XA, XR, XB, XD = WR, 2 * WR, WR + V, 2 * WR + V
+M1, M2, M4, M64 = 1.5 * 2 ** 23, 1.5 * 2 ** 24, 1.5 * 2 ** 25, 1.5 * 2 ** 29
+HUGE = float(2 ** 23)
+CSPLIT, BSPLIT = 2, 2
+F16 = "float16"
+
+SCRATCH = {}
+BUF = {}
+HOME = {}
+
+
+def _sb(name, cols, dtype):
+    BUF[name] = ("sbuf", [128] + (list(cols) if isinstance(cols, (list, tuple)) else [cols]), dtype)
+    if isinstance(cols, int) and cols <= 200:
+        pool = "pool_" + dtype
+        at = SCRATCH[pool][1][1] if pool in SCRATCH else 0
+        HOME[name] = (pool, at)
+        SCRATCH[pool] = ("sbuf", [128, at + (cols + 15) // 16 * 16], dtype)
+    else:
+        SCRATCH[name] = BUF[name]
+
+
+BF, F32, I32, U16 = "bfloat16", "float32", "int32", "uint16"
+_sb("X", 3 * WR + V, BF)
+for _nm, _c, _d in (
+        ("nti", 8, I32), ("ntf", 8, F32), ("wi", L, I32), ("di", L, I32), ("df", L, F32), ("zp", L, BF),
+        ("pi", 4, I32), ("pj", 4, I32), ("col", 8, F32), ("xi", 144, I32), ("xj", 128, I32), ("cw", 144, BF),
+        ("Pf", 5 * 128, F16), ("PI", 5 * 128, BF), ("PD", 4 * 128, BF), ("If", 128, F16), ("Ie", 128, F16),
+        ("I1", 128, BF), ("Id", 128, BF), ("I4", 128, BF), ("In", 128, BF), ("Ih", 128, BF),
+        ("B1", 128, BF), ("Y", 128, BF), ("MK", 16 * 128, BF), ("s1", 16, F32), ("s2", 16, F32),
+        ("Z1", 144, BF), ("Z65", 144, BF), ("Zu", 144, BF), ("Hf", 128, F32), ("Hg", 128, F32), ("Hh", 128, BF), ("Hl", 128, BF),
+        ("dl5", 5 * n, F32), ("dl16", 16 * C, F32), ("rmx", 16 * n, BF), ("rmn", 16 * n, BF),
+        ("ch", L, BF), ("c8", n, BF), ("b16", C, F32), ("b4", 12, BF), ("c2k", n, BF), ("cM1", L, BF), ("cM2", n, BF), ("cM4", n, BF),
+        ("c15", 12, BF), ("Bn", 128, BF), ("Zn", 144, BF),
+        ("SB", 4 * 5 * L, BF), ("LB", 3 * 5 * L, BF), ("SF", 3 * 2 * L, F32), ("LF", 3 * 2 * L, F32),
+        ("MS", 3 * L, BF), ("ML", 3 * L, BF), ("FW", 2 * L, F32), ("FS", 2 * L, F32), ("FL", 2 * L, F32), ("GL", L, BF),
+        ("Gh", 128, BF), ("Gl", 128, BF), ("cf", n, F32), ("cah", n, BF), ("cal", n, BF), ("cMv", n, BF),
+        ("nv", L, BF), ("dd", 12, BF), ("d2", 12, F32), ("sB", 12, F32),
+        ("uA", 12, U16), ("uB", 12, U16)):
+    _sb(_nm, _c, _d)
+for _k in range(NCH):
+    for _nm, _c, _d in (
+            ("fq", n, BF), ("T5", 5 * n, F32), ("ina", n, BF), ("x", n, F32), ("yi", n, I32), ("ixi", n, I32), ("ixu", n, U16),
+            ("bz", 32 * n, BF), ("shi", n, BF), ("slo", n, BF), ("sg", 15 * n, BF), ("wsg", [n, 16], BF),
+            ("sa", 16 * C, BF), ("ky", 16 * C, F32), ("ki", C, I32), ("kj", C, I32), ("ku", C, U16), ("sgm", 16 * n, BF), ("ry", n, F32),
+            ("hu", n, U16), ("cc", 16 * n, BF), ("mx", 16 * n, BF), ("mn", 16 * n, BF),
+            ("gf", n, BF), ("u3", 3 * n, BF), ("e2", 2 * n, BF), ("ah", 2 * n, F16)):
+        _sb("%s%d" % (_nm, _k), _c, _d)
+    BUF["wsx%d" % _k] = BUF["wsg%d" % _k]
+for _k in range(8):
+    SCRATCH["pb%d" % _k] = ("psum", [128, 512], F32)
+
+SEMAPHORES = ["sV", "sS", "sP", "sG", "sent", "ld0", "ld1", "ld2", "ld3", "ld4", "ld5", "stx", "stz", "finz"]
+for _k in range(NCH):
+    SEMAPHORES += ["fin%d" % _k, "sw%d" % _k, "sd%d" % _k]
+    for _t in range(RO):
+        SEMAPHORES += ["ma%d_%d" % (_t, _k), "mb%d_%d" % (_t, _k), "me%d_%d" % (_t, _k)]
+
+CY, CP, FIX, LAT, ISSUE = 0.00104, 0.00052, 0.06, 0.10, 0.8
+BYTES = {BF: 2, F32: 4, I32: 4, U16: 2, "float16": 2}
+
+
+def A(name, *ix):
+    return ("s", name, ix if ix else (slice(None),))
+
+
+def sl(name, lo, hi, st=1):
+    return ("s", name, (slice(lo, hi, st),))
+
+
+def ps(tile, lo, hi, st=1):
+    return ("p", tile, (slice(lo, hi, st),))
+
+
+def ind(win, off):
+    return ("i", win, off)
+
+
+def ext(name, lo, hi):
+    return ("x", name, (slice(lo, hi),))
+
+
+def span(ap):
+    shape = BUF[ap[1]][1][1:]
+    a = np.arange(int(np.prod(shape))).reshape(shape)[ap[2]]
+    return int(a.min()), int(a.max()) + 1, int(a.size)
+
+
+def count(ap):
+    if ap[0] == "i":
+        return 16 * span(ap[2])[2]
+    if ap[0] == "p":
+        return len(range(512)[ap[2][0]])
+    return span(ap)[2]
+
+
+def two(ap):
+    return ap[0] == "s" and BYTES[BUF[ap[1]][2]] == 2
+
+
+def build():
+    ops = []
+    tiles, now = [0], [None]
+    ALL = slice(None)
+
+    def tile():
+        tiles[0] += 1
+        return tiles[0]
+
+    def add(ways, outs, ins, sem=None, lat=0.0, val=16):
+        R, W, P = [], [], set()
+        for lst, aps in ((W, outs), (R, ins)):
+            for ap in aps:
+                if not isinstance(ap, tuple):
+                    continue
+                if ap[0] == "i":
+                    lst.append((ap[1][1],) + span(ap[1])[:2])
+                    R.append((ap[2][1],) + span(ap[2])[:2])
+                elif ap[0] == "p":
+                    P.add(ap[1])
+                elif ap[0] == "s":
+                    lst.append((ap[1],) + span(ap)[:2])
+        ops.append({"ways": ways, "R": R, "W": W, "P": P, "sem": sem, "lat": lat, "val": val, "tag": now[0],
+                    "PW": set(ap[1] for ap in outs if isinstance(ap, tuple) and ap[0] == "p")})
+
+    def vcost(out, ins, per):
+        k = count(out)
+        if out[0] == "i":
+            return FIX + 3.5 * k * CY
+        if ins and ins[0][0] == "i":
+            return FIX + 1.56 * k * CY
+        return FIX + max(64 * CY - FIX, 0, per * k * CY)
+
+    def half(aps):
+        return 0.5 if all(two(a) for a in aps) else 1.0
+
+    def w_ts(out, a, s1, op0, s2=None, op1=None):
+        args = (out, a, s1, s2, op0) + ((op1,) if op1 is not None else ())
+        return [("tensor_scalar", args, {})], vcost(out, [a], half([out, a]))
+
+    def w_act(out, a, f, bias=None, scale=None):
+        kw = {}
+        if bias is not None:
+            kw["bias"] = bias
+        if scale is not None:
+            kw["scale"] = scale
+        return [("activation", (out, a, f), kw)], vcost(out, [a], 1.0)
+
+    def w_cp(out, a):
+        return [("tensor_copy", (out, a), {})], vcost(out, [a], half([out, a]))
+
+    def ts(out, a, s1, op0, s2=None, op1=None):
+        add({"V": w_ts(out, a, s1, op0, s2, op1)}, [out], [a, s1, s2])
+
+    def tt(out, a, b, op):
+        add({"V": ([("tensor_tensor", (out, a, b, op), {})], vcost(out, [a], 1.0 if "p" in (a[0], b[0]) else 2.0))}, [out], [a, b])
+
+    def cp(out, a):
+        add({"V": w_cp(out, a)}, [out], [a])
+
+    def ms(out, v):
+        add({"V": ([("memset", (out, v), {})], vcost(out, [], half([out])))}, [out], [])
+
+    def scan(out, d0, d1, op0, op1):
+        add({"V": ([("tensor_tensor_scan", (out, d0, d1, 0.0, op0, op1), {})], vcost(out, [d0], half([out, d0, d1])))}, [out], [d0, d1])
+
+    def act(out, a, f, bias=None, scale=None):
+        add({"S": w_act(out, a, f, bias, scale)}, [out], [a])
+
+    def cp2(out, a):
+        add({"S": w_act(out, a, ACT.Copy), "V": w_cp(out, a)}, [out], [a])
+
+    def lin2(out, a, mul, plus):
+        add({"S": w_act(out, a, ACT.Identity if plus else ACT.Copy, plus if plus else None, mul if mul != 1.0 else None),
+             "V": w_ts(out, a, mul, ALU.mult, plus, ALU.add)}, [out], [a])
+
+    def sign2(out, a):
+        add({"S": w_act(out, a, ACT.Sign), "V": w_ts(out, a, 1.0, ALU.min, -1.0, ALU.max)}, [out], [a])
+
+    def mm(groups, also=()):
+        calls, outs, ins, cost = [], [], list(also), 0.03
+        for out, terms in groups:
+            outs.append(out)
+            for j, (l, r) in enumerate(terms):
+                calls.append(("matmul", (out, l, r, j == 0, j == len(terms) - 1), {}))
+                ins += [l, r]
+                cost += max(64, count(r)) * CP * (1 if two(r) else 4)
+        add({"P": (calls, cost)}, outs, ins)
+
+    def iota(out, pat, base, cm):
+        kw = {} if BUF[out[1]][2] == I32 else {"allow_small_or_imprecise_dtypes": True}
+        add({"G": ([("iota", (out, pat, base, cm), kw)], 0.13 + 2 * count(out) * CY)}, [out], [])
+
+    def dma(eng, out, a, sem, lat):
+        add({eng: ([("dma_start", (out, a), {})], 0.1 if eng != "G" else 1.0)}, [out], [a], sem=sem, lat=lat)
+
+    def send(kind, parts, sem, lat, high=False):
+        add({"G": ([("send", (kind, parts, sem, high), {})], ISSUE)}, [p[0] for p in parts], [p[1] for p in parts],
+            sem=sem, lat=lat, val=sum(p[2] for p in parts))
+
+    def blk(name, j):
+        return sl(name, 128 * j, 128 * j + 128)
+
+    def zk(name, k):
+        return sl(name, 15 - k, 143 - k)
+
+    def tri(name, t, k, j=None):
+        o = (t * NCH + k) * 5 * n
+        return sl(name, o, o + 3 * n) if j is None else sl(name, o + j, o + 3 * n, 3)
+
+    def duo(name, t, k, j=None):
+        o = (t * NCH + k) * 2 * n
+        return sl(name, o, o + 2 * n) if j is None else sl(name, o + j, o + 2 * n, 2)
+
+    def cut(name, t, k, j, parts=2):
+        o = (t * NCH + k) * parts * n
+        return sl(name, o, o + parts * n) if j is None else sl(name, o + j * n, o + j * n + n)
+
+    dma("S", sl("X", XA, XA + V), ext("xs", 0, V), "ld0", 6.0)
+    dma("Y", sl("nti", 0, D), ext("nt", 0, D), "ld1", 2.0)
+    dma("Y", A("di"), ext("d0", 0, L), "ld2", 2.0)
+    dma("Y", A("wi"), ext("w0", 0, L), "ld3", 2.0)
+    dma("Y", A("zp"), ext("z0", 0, L), "ld4", 2.0)
+    dma("Y", sl("X", XB, XD), ext("xs", 0, WR), "ld5", 6.0)
+    iota(sl("pi", 0, 1), [[0, 1]], 0, 1)
+    iota(A("xi"), [[1, 144]], 0, 0)
+    iota(A("dl5"), [[0, n], [-16384, 5]], 8192, 0)
+    ms(sl("dl5", 0, 5 * n, 5), HUGE)
+    for k in range(NCH):
+        for j in range(4):
+            iota(sl("bz%d" % k, 4 * n * j, 4 * n * (j + 1)), [[0, 4 * n]], 0, 0)
+    for j in range(4):
+        iota(sl("rmx", 4 * n * j, 4 * n * (j + 1)), [[0, n // 4], [2048, 16]], -1024, 0)
+        iota(sl("rmn", 4 * n * j, 4 * n * (j + 1)), [[0, n // 4], [-2048, 16]], 1024, 0)
+    g16, kc, c1, c2, c3, c16, c4 = (sl("col", j, j + 1) for j in range(7))
+    ts(sl("pj", 0, 1), sl("pi", 0, 1), 112, ALU.bitwise_and)
+    ts(sl("pj", 1, 2), sl("pi", 0, 1), 15, ALU.bitwise_and)
+    cp(sl("col", 0, 2), sl("pj", 0, 2))
+    ts(A("cw"), A("xi"), g16, ALU.subtract)
+    cm = sl("cw", 0, 128)
+    cp(sl("ntf", 0, D), sl("nti", 0, D))
+    ts(A("I1"), cm, kc, ALU.is_equal)
+    ts(A("Ie"), cm, kc, ALU.is_equal)
+    ts(A("If"), cm, kc, ALU.is_equal, 2080.0, ALU.mult)
+    for e in range(D):
+        ts(blk("Pf", e), cm, sl("ntf", e, e + 1), ALU.is_equal)
+    for es in ((0, 1, 2), (3, 4)):
+        pc = tile()
+        mm([(ps(pc, 128 * j, 128 * j + 128), [(blk("Pf", e), A("Ie")), (A("I1"), A("I1"))]) for j, e in enumerate(es)])
+        cp2(sl("PI", 128 * es[0], 128 * es[-1] + 128), ps(pc, 0, 128 * len(es)))
+        for j, e in enumerate(es):
+            if e < 4:
+                lin2(blk("PD", e), blk("PI", e), 8192.0 * (4 - e), 0.0)
+    lin2(A("Id"), A("I1"), 2464.0, 0.0)
+    lin2(A("I4"), A("I1"), 4.0, 0.0)
+    lin2(A("In"), A("I1"), -1.0, 0.0)
+    lin2(A("Ih"), A("I1"), 0.5, 0.0)
+    ts(A("xj"), sl("xi", 0, 128), 112, ALU.bitwise_and)
+    ts(A("B1"), A("xj"), g16, ALU.is_equal)
+    ts(A("Z1"), A("cw"), 15.0, ALU.is_equal)
+    lin2(A("Z65"), A("Z1"), 65.0, 0.0)
+    lin2(c1, kc, 4.0, 3.0)
+    lin2(c2, kc, 2.0, 1.0)
+    lin2(c3, kc, 333.0, -float(WR))
+    lin2(c16, kc, 16.0, 0.0)
+    lin2(c4, kc, 4.0, 0.0)
+    ts(A("Zu"), A("Z1"), c2, ALU.mult)
+    pc = tile()
+    mm([(ps(pc, 0, 128), [(A("I1"), A("I1")), (A("I1"), A("I1")), (A("In"), A("B1"))])])
+    cp2(A("Y"), ps(pc, 0, 128))
+    ts(A("s1"), sl("xi", 0, 16), kc, ALU.is_equal, -1.0, ALU.mult)
+    ts(A("s2"), sl("xi", 0, 16), kc, ALU.not_equal)
+    for k in range(15):
+        ts(blk("MK", k), A("Y"), sl("s1", k, k + 1), ALU.max, sl("s2", k, k + 1), ALU.min)
+    ts(A("Hf"), cm, c1, ALU.mult, c2, ALU.add)
+    tt(A("Hg"), A("Hf"), A("B1"), ALU.mult)
+    cp2(A("Hh"), A("Hg"))
+    tt(A("Hl"), A("Hg"), A("Hh"), ALU.subtract)
+    ms(A("dl16"), 1.0)
+    ms(sl("dl16", 0, 16 * C, 16), HUGE)
+    ms(sl("dl16", 15, 16 * C, 16), float(16 * n))
+    for nm, v in (("c8", -8.5), ("c2k", 2080.0), ("cM1", M1), ("cM2", M2), ("cM4", M4), ("c15", 1.5)):
+        ms(A(nm), v)
+    act(A("ch"), A("cM1"), ACT.Sigmoid, bias=-math.log(3.0), scale=0.0)
+    ops[-1]["ways"]["S"] = (ops[-1]["ways"]["S"][0], ops[-1]["ways"]["S"][1] + 1.5)
+    ops[-1]["first"] = True
+    lin2(A("Bn"), A("B1"), -1.0, 0.0)
+    lin2(A("Zn"), A("Zu"), -1.0, 0.0)
+    for k in range(NCH):
+        ms(cut("SB", 0, k, 4, 5), 0.0)
+    lin2(A("Gh"), A("Hh"), -1.0, 0.0)
+    lin2(A("Gl"), A("Hl"), -1.0, 0.0)
+    ms(A("cMv"), 4096.0 * M1)
+    ts(A("cf"), A("ch", slice(0, n)), 8190.0, ALU.mult, c3, ALU.subtract)
+    cp2(A("cah"), A("cf"))
+    tt(A("cal"), A("cf"), A("cah"), ALU.subtract)
+    ts(A("b16"), sl("xi", 0, C), 256.0, ALU.mult, c16, ALU.add)
+    ts(A("b4"), sl("xi", 0, L // 16), 64.0, ALU.mult, c4, ALU.add)
+    for k in range(NCH):
+        ms(A("u3%d" % k), 1.0)
+        ms(sl("u3%d" % k, 0, 3 * n, 3), 0.0)
+        ms(A("e2%d" % k), 0.0)
+    cp(A("df"), A("di"))
+    for k in range(NCH):
+        now[0] = k
+        cp2(tri("SB", 0, k, 2), sl("df", k * n, k * n + n))
+        ts(sl("ah%d" % k, 1, 2 * n, 2), sl("wi", k * n, k * n + n), -2048.0, ALU.add)
+
+    def phase_a(t, k):
+        now[0] = k
+
+        def b(nm, lo=None, hi=None, st=1):
+            return A("%s%d" % (nm, k)) if lo is None else sl("%s%d" % (nm, k), lo, hi, st)
+        d, ah, a = tri("SB", t, k, 2), b("ah", 1, 2 * n, 2), duo("SF", t, k, 1)
+        z = sl("zp", k * n, k * n + n) if t == 0 else cut("ML", t - 1, k, 0, 1)
+        m = cut("MS", t, k, 0, 1)
+        act(b("fq"), d, ACT.Square, bias=-256.0, scale=64.0)
+        p0, p2 = tile(), tile()
+        mm([(ps(p0, e, 5 * n, 5), [(blk("Pf", e), ah)] + ([(blk("PD", e), d)] if e < 4 else []) + [(blk("PI", e), b("fq"))]) for e in range(D)])
+        mm([(ps(p2, 0, n), [(A("If"), ah), (A("Id"), d)]), (ps(p2, n, 2 * n), [(A("Ie"), ah), (A("I1"), A("c2k"))]), (ps(p2, 2 * n, 3 * n), [(A("Ie"), ah)])])
+        cp2(a, ps(p2, 2 * n, 3 * n))
+        scan(b("T5"), A("dl5"), ps(p0, 0, 5 * n), ALU.add, ALU.min)
+        Tp = b("T5", 4, 5 * n, 5)
+        tt(b("x"), ps(p2, n, 2 * n), Tp, ALU.mult)
+        tt(b("yi"), ps(p2, 0, n), b("x"), ALU.add)
+        tt(duo("SF", t, k, 0), Tp, ps(p2, 2 * n, 3 * n), ALU.subtract)
+        ts(b("ina"), Tp, 2048.0, ALU.is_ge, 4080.0, ALU.mult)
+        ts(b("ixi"), b("yi"), 5, ALU.arith_shift_right, V - 1, ALU.bitwise_and)
+        cp(b("ixu"), b("ixi"))
+        h = n // BSPLIT
+        for j in range(BSPLIT):
+            cp2(b("bz", 16 * n + 16 * h * j, 16 * n + 16 * h * (j + 1)), ind(sl("X", XA, XA + V), b("ixu", h * j, h * j + h)))
+        cp2(b("bz", 0, 16 * n, 16), z)
+        pw = tile()
+        w = A("wsg%d" % k, ALL, 15)
+        mm([(ps(pw, 0, n), [(A("I1"), d), (A("I1"), b("ina"))])])
+        act(w, ps(pw, 0, n), ACT.Sigmoid, bias=-30.0 * math.log(2.0), scale=-math.log(2.0))
+        if t > 0:
+            pa = tile()
+            hit = tri("SB", t, k, 1)
+            mm([(ps(pa, 0, n), [(A("B1"), hit), (A("I1"), A("cM4")), (A("In"), A("cM4")), (A("Bn"), hit)])])
+            act(cut("SB", t, k, 4, 5), ps(pa, 0, n), ACT.Abs)
+        p3 = tile()
+        s = ps(p3, 0, n)
+        mm([(s, [(A("I4"), b("ina"))] + [(zk("Z1", j), b("bz", 16 * n + j, 32 * n, 16)) for j in range(16)])])
+        cp2(b("shi"), s)
+        tt(b("slo"), s, b("shi"), ALU.subtract)
+        po = tile()
+        mm([(ps(po, 0, n), [(A("I1"), b("shi")), (A("I1"), b("slo")), (A("I1"), A("cM2")), (A("In"), A("cM2")), (A("In"), b("shi")), (A("In"), b("slo"))])])
+        act(cut("SB", t, k, 3, 5), ps(po, 0, n), ACT.Abs)
+        send("next", [(duo("LF", t, k), duo("SF", t, k), 8, 0 if t + k == 0 else 2)], "me%d_%d" % (t, k), 6.0)
+        pr = tile()
+        mm([(ps(pr, j, SL * n, SL), [(A("I1"), w)]) for j in range(SL)])
+        for q in range(15 // SL):
+            pd = tile()
+            sg = b("sg", q * SL * n, (q + 1) * SL * n)
+            mm([(ps(pd, j, SL * n, SL), [(blk("MK", 14 - q * SL - j), b("shi")), (blk("MK", 14 - q * SL - j), b("slo"))]) for j in range(SL)])
+            sign2(sg, ps(pd, 0, SL * n))
+            tt(A("wsx%d" % k, ALL, slice(q * SL, q * SL + SL)), ps(pr, 0, SL * n), sg, ALU.mult)
+        p4 = tile()
+        mm([(ps(p4, 0, 16 * C), [(zk("Z1", j), A("wsg%d" % k, slice(j, n, 16), ALL)) for j in range(16)])], [A("wsx%d" % k)])
+        act(b("sa"), ps(p4, 0, 16 * C), ACT.Abs, scale=float(2 ** 45))
+        scan(b("ky"), A("dl16"), b("sa"), ALU.add, ALU.min)
+        tt(b("ki"), b("ky", 15, 16 * C, 16), A("b16"), ALU.add)
+        ts(b("kj"), b("ki"), V - 1, ALU.bitwise_and)
+        cp(b("ku"), b("kj"))
+        cp2(m, ind(b("bz"), b("ku")))
+        send("next", [(cut("ML", t, k, 0, 1), m, 8, 0)], "ma%d_%d" % (t, k), 4.0)
+        ts(sl("dd", k * C, k * C + C), b("ky", 15, 16 * C, 16), 0.5, ALU.is_ge, float(WR), ALU.mult)
+        for q in range(16 // SG):
+            pd = tile()
+            mm([(ps(pd, j * n, j * n + n), [(A("I1"), b("bz", 16 * n + q * SG + j, 32 * n, 16)), (A("In"), m)]) for j in range(SG)])
+            act(b("sgm", q * SG * n, (q + 1) * SG * n), ps(pd, 0, SG * n), ACT.Sigmoid, bias=-math.log(64.0), scale=40.0)
+        p5 = tile()
+        y, hp = ps(p5, 0, n), ps(p5, n, 2 * n)
+        mm([(y, [(A("I1"), b("ina")), (A("I1"), A("c8"))] + [(zk("Z65", j), b("sgm", j * n, j * n + n)) for j in range(16)])])
+        ts(b("ry"), y, M64, ALU.add, M64, ALU.subtract)
+        ts(hp, y, 480.0, ALU.is_lt)
+        tt(tri("SB", t, k, 1), y, b("ry"), ALU.is_ge)
+        tt(tri("SB", t, k, 0), hp, tri("SB", t, k, 1), ALU.subtract)
+        send("next", [(cut("LB", t, k, None, 5), cut("SB", t, k, None, 5), 8, 1)], "mb%d_%d" % (t, k), 5.5)
+
+    def writes(t):
+        now[0] = None
+        m = sl("MS", t * L, t * L + L)
+        z = A("zp") if t == 0 else sl("ML", (t - 1) * L, t * L)
+        p6 = tile()
+        u = ps(p6, L, L + 12)
+        mj = [sl("MS", t * L + j, t * L + L, 16) for j in range(16)]
+        p7 = tile()
+        mm([(ps(p7, 0, L), [(A("Ih"), m), (A("Ih"), z), (A("In"), A("ch")), (A("I1"), A("cM1")), (A("In"), A("cM1"))])])
+        mm([(u, [(zk("Zn", j), mj[j]) for j in range(16)] + [(A("I1"), A("c15")), (A("I1"), sl("cM4", 0, 12)), (A("In"), sl("cM4", 0, 12))]
+             + [(zk("Zu", j), mj[j]) for j in range(16)] + [(A("I1"), A("b4")), (A("I1"), A("dd"))])])
+        cp2(A("nv"), ps(p7, 0, L))
+        cp(A("uA"), u)
+        cp(ind(sl("X", 0, XR), A("uA")), A("nv"))
+        if t < RO - 1:
+            ts(A("d2"), A("dd"), -2.0, ALU.mult, float(WR), ALU.add)
+            tt(A("sB"), u, A("d2"), ALU.add)
+            cp(A("uB"), A("sB"))
+
+    def phase_b(t, k):
+        now[0] = k
+
+        def b(nm, lo=None, hi=None, st=1):
+            return A("%s%d" % (nm, k)) if lo is None else sl("%s%d" % (nm, k), lo, hi, st)
+        m = cut("ML", t, k, 0, 1)
+        p0 = tile()
+        mm([(ps(p0, 0, n), [(A("I1"), A("cah")), (A("I1"), A("cal")), (A("Gh"), m), (A("Gl"), m), (A("I1"), A("cMv")), (A("In"), A("cMv")),
+                            (A("Hh"), m), (A("Hl"), m)])])
+        ts(b("hu"), ps(p0, 0, n), c3, ALU.add)
+        h = n // CSPLIT
+        for j in range(CSPLIT):
+            lo, hi = 16 * h * j, 16 * h * (j + 1)
+            cp2(b("cc", lo, hi), ind(sl("X", XR, XR + V), b("hu", h * j, h * j + h)))
+            scan(b("mx", lo, hi), sl("rmx", lo, hi), b("cc", lo, hi), ALU.min, ALU.max)
+            scan(b("mn", lo, hi), sl("rmn", lo, hi), b("cc", lo, hi), ALU.max, ALU.min)
+        p1 = tile()
+        mm([(ps(p1, 0, n), [(A("In"), m), (A("In"), m), (A("I1"), b("mx", 15, 16 * n, 16)), (A("I1"), b("mn", 15, 16 * n, 16))])])
+        act(b("gf"), ps(p1, 0, n), ACT.Sign, bias=-1.5)
+        p2 = tile()
+        ap_ = cut("LB", t, k, 4, 5)
+        mm([(ps(p2, 0, n), ([(A("In"), ap_)] if t > 0 else []) + [(A("B1"), b("gf"))])])
+        ts(b("u3", 1, 3 * n, 3), ps(p2, 0, n), -0.5, ALU.is_ge)
+        scan(tri("SB", t + 1, k), b("u3"), tri("LB", t, k), ALU.mult, ALU.add)
+        p3 = tile()
+        mm([(ps(p3, 0, n), [(A("In"), cut("LB", t, k, 3, 5)), (A("I1"), b("u3", 1, 3 * n, 3)), (A("I4"), tri("SB", t + 1, k, 1))])])
+        ts(b("e2", 1, 2 * n, 2), ps(p3, 0, n), 4.0, ALU.is_equal)
+        scan(b("ah") if t < RO - 1 else duo("FW", 0, k), b("e2"), duo("LF", t, k), ALU.mult, ALU.add)
+
+    for t in range(RO):
+        for k in range(NCH):
+            phase_a(t, k)
+        writes(t)
+        for k in range(NCH):
+            phase_b(t, k)
+        now[0] = None
+        if t < RO - 1:
+            cp(ind(sl("X", XB, XD + WR), A("uB")), A("nv"))
+    dma("Y", ext("xn", 0, WR), sl("X", XA, XR), "stx", 2.5)
+    send("home", [(A("GL"), sl("ML", (RO - 1) * L, RO * L), 8, 1)], "finz", 5.0)
+    dma("Y", ext("zn", 0, L), A("GL"), "stz", 2.0)
+    for k in range(NCH):
+        now[0] = k
+        cp2(cut("FS", 0, k, 1), tri("SB", RO, k, 2))
+        lin2(cut("FS", 0, k, 0), duo("FW", 0, k, 1), 1.0, 2048.0)
+        send("home", [(cut("FL", 0, k, j), cut("FS", 0, k, j), 4, 2 * j) for j in range(2)], "fin%d" % k, 4.5)
+    for k in range(NCH):
+        now[0] = k
+        dma("Y", ext("wn", k * n, k * n + n), cut("FL", 0, k, 0), "sw%d" % k, 2.0)
+        dma("Y" if k < NCH - 1 else "S", ext("dn", k * n, k * n + n), cut("FL", 0, k, 1), "sd%d" % k, 2.0)
+    byname, bytile = {}, {}
+    for i, o in enumerate(ops):
+        deps = set()
+        names = set(r[0] for r in o["R"] + o["W"])
+        for j in set(j for nm in names for j in byname.get(nm, [])):
+            p = ops[j]
+            if hits(o["R"], p["W"]) or hits(o["W"], p["W"]) or hits(o["W"], p["R"]):
+                deps.add(j)
+        for tl in o["P"]:
+            for j in bytile.get(tl, []):
+                p = ops[j]
+                if len(p["ways"]) > 1 or list(p["ways"]) != list(o["ways"]) or tl in p["PW"] or tl in o["PW"]:
+                    deps.add(j)
+            bytile.setdefault(tl, []).append(i)
+        for nm in names:
+            byname.setdefault(nm, []).append(i)
+        o["deps0"] = deps
+        o["only"] = list(o["ways"])[0]
+    return ops, bytile
+
+
+def hits(x, y):
+    return any(a[0] == b[0] and a[1] < b[2] and b[1] < a[2] for a in x for b in y)
+
+
+def schedule(ops, bytile, win, stag, lift, vpen):
+    N_ = len(ops)
+    succ = [[] for _ in ops]
+    for i, o in enumerate(ops):
+        o["deps"] = set(o["deps0"])
+        o["inc"] = False
+        for j in o["deps"]:
+            succ[j].append(i)
+    rank = [0.0] * N_
+    for i in range(N_ - 1, -1, -1):
+        rank[i] = min(w[1] for w in ops[i]["ways"].values()) + ops[i]["lat"] + max([LAT + rank[j] for j in succ[i]] + [0.0])
+        rank[i] += 100.0 if ops[i].get("first") else 0.0
+    prio = [rank[i] - stag * (ops[i]["tag"] or 0) + lift[i] for i in range(N_)]
+    free = {e: 0.0 for e in "VSPGY"}
+    end, order, at = {}, [], {}
+    left = [len(o["deps"]) for o in ops]
+    ready = [i for i in range(N_) if left[i] == 0]
+    for i in ready:
+        at[i] = 0.0
+    bank, holder, togo = {}, [None] * 8, {tl: len(v) for tl, v in bytile.items()}
+    while ready:
+        cand = [(max([end[j] for j in bytile[holder[b_]]]) + LAT if holder[b_] is not None else 0.0, b_)
+                for b_ in range(8) if holder[b_] is None or togo[holder[b_]] == 0]
+        opts = []
+        for i in ready:
+            o = ops[i]
+            st, pick = at[i], None
+            new = [tl for tl in o["P"] if tl not in bank]
+            if new:
+                if len(cand) < (2 if "P" in o["ways"] else 1):
+                    continue
+                pick = min(cand)
+                st = max(st, pick[0])
+            if len(o["ways"]) == 1:
+                e = o["only"]
+            else:
+                e = "V" if max(st, free["V"]) + o["ways"]["V"][1] + vpen[i] < max(st, free["S"]) + o["ways"]["S"][1] else "S"
+            opts.append((max(st, free[e]), i, e, pick, new))
+        if not opts:
+            return None, None, 1e9
+        t0 = min(x[0] for x in opts)
+        st, i, e, pick, new = max((x for x in opts if x[0] <= t0 + win), key=lambda x: prio[x[1]])
+        o = ops[i]
+        if new:
+            if holder[pick[1]] is not None:
+                o["deps"] |= set(bytile[holder[pick[1]]])
+            holder[pick[1]] = new[0]
+            bank[new[0]] = pick[1]
+        for tl in o["P"]:
+            togo[tl] -= 1
+        o["eng"], o["calls"], o["cost"], o["start"] = e, o["ways"][e][0], o["ways"][e][1], st
+        free[e] = st + o["cost"]
+        end[i] = st + o["cost"] + o["lat"]
+        order.append(i)
+        ready.remove(i)
+        for j in succ[i]:
+            left[j] -= 1
+            if left[j] == 0:
+                ready.append(j)
+                at[j] = max(end[x] for x in ops[j]["deps0"]) + LAT
+    return order, bank, max(end.values())
+
+
+def plan(win, stag, pen, rounds, seed):
+    ops, bytile = build()
+    rng = np.random.default_rng(seed)
+    N_ = len(ops)
+    lift, vpen = [0.0] * N_, [pen] * N_
+    both = [i for i in range(N_) if len(ops[i]["ways"]) > 1 and ops[i]["ways"]["S"][1] > 0.3]
+    best = schedule(ops, bytile, win, stag, lift, vpen)[2]
+    for _ in range(rounds):
+        l2, v2 = list(lift), list(vpen)
+        kind = int(rng.integers(0, 3))
+        if kind == 0:
+            lo, up = int(rng.integers(0, N_)), float(rng.normal()) * 3.0
+            for i in range(lo, min(N_, lo + int(rng.integers(1, 30)))):
+                l2[i] += up
+        elif kind == 1:
+            for i in rng.integers(0, N_, 8):
+                l2[int(i)] += float(rng.normal()) * 2.0
+        else:
+            for i in rng.integers(0, len(both), 2):
+                v2[both[int(i)]] = float(rng.choice([-1.0, 0.0, 0.5, 1.5, 9.0]))
+        got = schedule(ops, bytile, win, stag, l2, v2)[2]
+        if got <= best:
+            best, lift, vpen = got, l2, v2
+    order, bank, total = schedule(ops, bytile, win, stag, lift, vpen)
+    pos = {i: x for x, i in enumerate(order)}
+    last = {}
+    for i in order:
+        o = ops[i]
+        need = {}
+        for j in o["deps"]:
+            p = ops[j]
+            if p["sem"] is None:
+                if p["eng"] == "P" and o["eng"] == "P":
+                    continue
+                if p["eng"] not in need or pos[j] > pos[need[p["eng"]]]:
+                    need[p["eng"]] = j
+            else:
+                need[p["sem"]] = j
+        o["need"] = []
+        for key, j in sorted(need.items()):
+            if pos[j] > last.get((o["eng"], key), -1):
+                last[(o["eng"], key)] = pos[j]
+                o["need"].append(j)
+                ops[j]["inc"] = True
+    cnt = {}
+    for i in order:
+        o = ops[i]
+        if o["sem"] is None and o["inc"]:
+            cnt[o["eng"]] = cnt.get(o["eng"], 0) + 1
+            o["sig"] = ("s" + o["eng"], cnt[o["eng"]])
+        elif o["sem"] is not None:
+            o["sig"] = (o["sem"], o["val"])
+    return ops, order, bank, total
+
+
+PLAN = plan(0.08, 2.0, 1.0, 1500, 0)
+
+
+def helpers(topo, src, dst):
+    c = [x for x in topo.cores_of(src) if x != src and topo.may_write(x, dst)]
+    return [x for x in c if topo.die(x) == topo.die(src)] + [x for x in c if topo.die(x) != topo.die(src)]
+
+
+def route(T, topo, r, kind, which):
+    src = T.cores[r]
+    dst = T.cores[(r - RO) % NR] if kind == "home" else T.cores[(r + 1) % NR]
+    return dst, (dst if topo.may_write(src, dst) else helpers(topo, src, dst)[which])
+
+
+def rank_program(g, core, T, topo):
+    ops, order, bank, _ = PLAN
+
+    def res(ap):
+        if not isinstance(ap, tuple):
+            return ap
+        if ap[0] == "i":
+            return res(ap[1]).indirect(res(ap[2]))
+        if ap[0] == "p":
+            return T["pb%d" % bank[ap[1]]][(slice(None),) + ap[2]]
+        if ap[1] in HOME:
+            pool, at = HOME[ap[1]]
+            lo, hi, st = ap[2][0].indices(BUF[ap[1]][1][1])
+            return T[pool][:, at + lo:at + hi:st] if st != 1 else T[pool][:, at + lo:at + hi]
+        return T[ap[1].replace("wsx", "wsg")][(slice(None),) + tuple(slice(x.start, x.stop) if isinstance(x, slice) and x.step == 1 else x for x in ap[2])]
+
+    def write(parts, sem, high):
+        tr, used = [], 0
+        for to, d_, s_, ne in parts:
+            eng = topo.engines(core, to)
+            eng = eng[::-1] if high else eng
+            tr.append((topo.addr(to, core), sum(1 << e for e in eng[used:used + ne]), res(d_), res(s_)))
+            used += ne
+        if len(tr) == 1:
+            g.remote_dma(tr[0][2], tr[0][3], T.sem[sem], T.sem.sent, tr[0][0][1], tr[0][0][0], tr[0][1])
+        else:
+            g.remote_dma_fused([RemoteDMATransfer(dst_ids=[DstId(rid=a_[0], pnc=a_[1])], dma_engine_mask=mk, remote_sem=T.sem[sem], src=s_, dst=d_)
+                                for a_, mk, d_, s_ in tr], local_sem=T.sem.sent)
+        return used
+
+    rank = T.rank_of(core)
+    sent = 0
+    if rank is None:
+        for i in order:
+            name, args, kw = ops[i]["calls"][0]
+            if name != "send":
+                continue
+            for r in range(NR):
+                mine = [(route(T, topo, r, args[0], p[3])[0], p[0], p[0], p[2]) for p in args[1] if route(T, topo, r, args[0], p[3])[1] == core]
+                if mine:
+                    g.wait_ge(T.sem[args[2]], sum(p[3] for p in mine))
+                    sent += write(mine, args[2], False)
+        if sent:
+            g.wait_ge(T.sem.sent, sent)
+        return
+    Q = {"V": g.vector, "S": g.scalar, "P": g.tensor, "G": g, "Y": g.sync}
+    call = {
+        "tensor_scalar": g.vector.tensor_scalar, "tensor_tensor": g.vector.tensor_tensor, "tensor_copy": g.vector.tensor_copy,
+        "memset": g.vector.memset, "tensor_tensor_scan": g.vector.tensor_tensor_scan, "activation": g.scalar.activation,
+        "matmul": g.tensor.matmul, "iota": g.iota}
+    tail = []
+    for i in order:
+        o = ops[i]
+        q = Q[o["eng"]]
+        for j in o["need"]:
+            q.wait_ge(T.sem[ops[j]["sig"][0]], ops[j]["sig"][1])
+        ins = None
+        for name, args, kw in o["calls"]:
+            if name == "send":
+                sent += write([(route(T, topo, rank, args[0], p[3])[1], p[0], p[1], p[2]) for p in args[1]], args[2], args[3])
+            elif name == "dma_start":
+                q.dma_start(res(args[0]), res(args[1])).then_inc(T.sem[o["sem"]], 16)
+                if not o["inc"]:
+                    tail.append(o["sem"])
+            else:
+                ins = call[name](*[res(x) for x in args], **kw)
+        if ins is not None and o["inc"]:
+            ins.then_inc(T.sem[o["sig"][0]], 1)
+    g.wait_ge(T.sem.sent, sent)
+    for s_ in tail:
+        g.wait_ge(T.sem[s_], 16)

@@ -1,6 +1,5 @@
 import math
 import numpy as np
-from concourse.bass import DstId, RemoteDMATransfer
 from concourse.mybir import AluOpType as ALU
 from concourse.mybir import ActivationFunctionType as ACT
 
@@ -10,7 +9,8 @@ n = L // NCH
 C = n // 16
 SL, SG = 5, 8
 WR = 4 * L
-XA, XR, XB, XD = WR, 2 * WR, WR + V, 2 * WR + V
+KP, UW = 4, L + 12
+KLAT, ULAT = 9.0, 5.5
 M1, M2, M4, M64 = 1.5 * 2 ** 23, 1.5 * 2 ** 24, 1.5 * 2 ** 25, 1.5 * 2 ** 29
 HUGE = float(2 ** 23)
 CSPLIT, BSPLIT = 2, 2
@@ -33,7 +33,8 @@ def _sb(name, cols, dtype):
 
 
 BF, F32, I32, U16 = "bfloat16", "float32", "int32", "uint16"
-_sb("X", 3 * WR + V, BF)
+for _k in range(RO + 1):
+    _sb("X%d" % _k, WR + V, BF)
 for _nm, _c, _d in (
         ("nti", 8, I32), ("ntf", 8, F32), ("wi", L, I32), ("di", L, I32), ("df", L, F32), ("zp", L, BF),
         ("pi", 4, I32), ("pj", 4, I32), ("col", 8, F32), ("xi", 144, I32), ("xj", 128, I32), ("cw", 144, BF),
@@ -44,11 +45,10 @@ for _nm, _c, _d in (
         ("dl5", 5 * n, F32), ("dl16", 16 * C, F32), ("rmx", 16 * n, BF), ("rmn", 16 * n, BF),
         ("ch", L, BF), ("c8", n, BF), ("b16", C, F32), ("b4", 12, BF), ("c2k", n, BF), ("cM1", L, BF), ("cM2", n, BF), ("cM4", n, BF),
         ("c15", 12, BF), ("Bn", 128, BF), ("Zn", 144, BF),
-        ("SB", 4 * 5 * L, BF), ("LB", 3 * 5 * L, BF), ("SF", 3 * 2 * L, F32), ("LF", 3 * 2 * L, F32),
-        ("MS", 3 * L, BF), ("ML", 3 * L, BF), ("FW", 2 * L, F32), ("FS", 2 * L, F32), ("FL", 2 * L, F32), ("GL", L, BF),
+        ("SB", 4 * 5 * L, BF), ("SF", 3 * 2 * L, F32), ("MS", 3 * L, BF), ("FW", 2 * L, F32), ("FS", 2 * L, F32),
+        ("US", 3 * UW, F32), ("UL", 7 * UW, F32), ("uo", 64, U16),
         ("Gh", 128, BF), ("Gl", 128, BF), ("cf", n, F32), ("cah", n, BF), ("cal", n, BF), ("cMv", n, BF),
-        ("nv", L, BF), ("dd", 12, BF), ("d2", 12, F32), ("sB", 12, F32),
-        ("uA", 12, U16), ("uB", 12, U16)):
+        ("dd", 12, BF)):
     _sb(_nm, _c, _d)
 for _k in range(NCH):
     for _nm, _c, _d in (
@@ -62,13 +62,13 @@ for _k in range(NCH):
 for _k in range(8):
     SCRATCH["pb%d" % _k] = ("psum", [128, 512], F32)
 
-SEMAPHORES = ["sV", "sS", "sP", "sG", "sent", "ld0", "ld1", "ld2", "ld3", "ld4", "ld5", "stx", "stz", "finz"]
+SEMAPHORES = ["sV", "sS", "sP", "sG", "sent", "ld0", "ld1", "ld2", "ld3", "stx", "stz"] + ["u%d" % _k for _k in range(7)]
 for _k in range(NCH):
-    SEMAPHORES += ["fin%d" % _k, "sw%d" % _k, "sd%d" % _k]
-    for _t in range(RO):
-        SEMAPHORES += ["ma%d_%d" % (_t, _k), "mb%d_%d" % (_t, _k), "me%d_%d" % (_t, _k)]
+    SEMAPHORES += ["sw%d" % _k, "sd%d" % _k]
+for _k in range(KP):
+    SEMAPHORES += ["lx%d" % _k] + ["k%d_%d" % (_c, _k) for _c in (1, 2, 3)] + ["left_k%d_%d" % (_c, _k) for _c in (1, 2, 3)]
 
-CY, CP, FIX, LAT, ISSUE = 0.00104, 0.00052, 0.06, 0.10, 0.8
+CY, CP, FIX, LAT, ISSUE = 0.00095, 0.00048, 0.06, 0.10, 1.0
 BYTES = {BF: 2, F32: 4, I32: 4, U16: 2, "float16": 2}
 
 
@@ -206,8 +206,8 @@ def build():
     def dma(eng, out, a, sem, lat):
         add({eng: ([("dma_start", (out, a), {})], 0.1 if eng != "G" else 1.0)}, [out], [a], sem=sem, lat=lat)
 
-    def send(kind, parts, sem, lat, high=False):
-        add({"G": ([("send", (kind, parts, sem, high), {})], ISSUE)}, [p[0] for p in parts], [p[1] for p in parts],
+    def send(kind, parts, sem, lat, high=False, also=()):
+        add({"G": ([("send", (kind, parts, sem, high), {})], ISSUE)}, [p[0] for p in parts], [p[1] for p in parts] + list(also),
             sem=sem, lat=lat, val=sum(p[2] for p in parts))
 
     def blk(name, j):
@@ -228,12 +228,14 @@ def build():
         o = (t * NCH + k) * parts * n
         return sl(name, o, o + parts * n) if j is None else sl(name, o + j * n, o + j * n + n)
 
-    dma("S", sl("X", XA, XA + V), ext("xs", 0, V), "ld0", 6.0)
-    dma("Y", sl("nti", 0, D), ext("nt", 0, D), "ld1", 2.0)
-    dma("Y", A("di"), ext("d0", 0, L), "ld2", 2.0)
-    dma("Y", A("wi"), ext("w0", 0, L), "ld3", 2.0)
-    dma("Y", A("zp"), ext("z0", 0, L), "ld4", 2.0)
-    dma("Y", sl("X", XB, XD), ext("xs", 0, WR), "ld5", 6.0)
+    for j, (eng, out, src, lat) in enumerate((("Y", sl("nti", 0, D), ext("nt", 0, D), 2.2), ("S", A("di"), ext("d0", 0, L), 2.2),
+                                              ("Y", A("wi"), ext("w0", 0, L), 2.2))):
+        dma(eng, out, src, "ld%d" % j, lat)
+        ops[-1]["first"] = 9 - j
+    for j in range(KP):
+        dma("Y", sl("X0", WR + j * V // KP, WR + (j + 1) * V // KP), ext("xs", j * V // KP, (j + 1) * V // KP), "lx%d" % j, 2.5 + 4.0 * (j + 1) / KP)
+        ops[-1]["first"] = 5 - j
+    dma("Y", A("zp"), ext("z0", 0, L), "ld3", 7.0)
     iota(sl("pi", 0, 1), [[0, 1]], 0, 1)
     iota(A("xi"), [[1, 144]], 0, 0)
     iota(A("dl5"), [[0, n], [-16384, 5]], 8192, 0)
@@ -273,7 +275,7 @@ def build():
     lin2(A("Z65"), A("Z1"), 65.0, 0.0)
     lin2(c1, kc, 4.0, 3.0)
     lin2(c2, kc, 2.0, 1.0)
-    lin2(c3, kc, 333.0, -float(WR))
+    lin2(c3, kc, 333.0, 0.0)
     lin2(c16, kc, 16.0, 0.0)
     lin2(c4, kc, 4.0, 0.0)
     ts(A("Zu"), A("Z1"), c2, ALU.mult)
@@ -298,11 +300,9 @@ def build():
     ops[-1]["first"] = True
     lin2(A("Bn"), A("B1"), -1.0, 0.0)
     lin2(A("Zn"), A("Zu"), -1.0, 0.0)
-    for k in range(NCH):
-        ms(cut("SB", 0, k, 4, 5), 0.0)
     lin2(A("Gh"), A("Hh"), -1.0, 0.0)
     lin2(A("Gl"), A("Hl"), -1.0, 0.0)
-    ms(A("cMv"), 4096.0 * M1)
+    ms(A("cMv"), V * M1)
     ts(A("cf"), A("ch", slice(0, n)), 8190.0, ALU.mult, c3, ALU.subtract)
     cp2(A("cah"), A("cf"))
     tt(A("cal"), A("cf"), A("cah"), ALU.subtract)
@@ -324,7 +324,7 @@ def build():
         def b(nm, lo=None, hi=None, st=1):
             return A("%s%d" % (nm, k)) if lo is None else sl("%s%d" % (nm, k), lo, hi, st)
         d, ah, a = tri("SB", t, k, 2), b("ah", 1, 2 * n, 2), duo("SF", t, k, 1)
-        z = sl("zp", k * n, k * n + n) if t == 0 else cut("ML", t - 1, k, 0, 1)
+        z = sl("zp", k * n, k * n + n) if t == 0 else cut("MS", t - 1, k, 0, 1)
         m = cut("MS", t, k, 0, 1)
         act(b("fq"), d, ACT.Square, bias=-256.0, scale=64.0)
         p0, p2 = tile(), tile()
@@ -341,7 +341,7 @@ def build():
         cp(b("ixu"), b("ixi"))
         h = n // BSPLIT
         for j in range(BSPLIT):
-            cp2(b("bz", 16 * n + 16 * h * j, 16 * n + 16 * h * (j + 1)), ind(sl("X", XA, XA + V), b("ixu", h * j, h * j + h)))
+            cp2(b("bz", 16 * n + 16 * h * j, 16 * n + 16 * h * (j + 1)), ind(sl("X%d" % t, WR, WR + V), b("ixu", h * j, h * j + h)))
         cp2(b("bz", 0, 16 * n, 16), z)
         pw = tile()
         w = A("wsg%d" % k, ALL, 15)
@@ -360,7 +360,6 @@ def build():
         po = tile()
         mm([(ps(po, 0, n), [(A("I1"), b("shi")), (A("I1"), b("slo")), (A("I1"), A("cM2")), (A("In"), A("cM2")), (A("In"), b("shi")), (A("In"), b("slo"))])])
         act(cut("SB", t, k, 3, 5), ps(po, 0, n), ACT.Abs)
-        send("next", [(duo("LF", t, k), duo("SF", t, k), 8, 0 if t + k == 0 else 2)], "me%d_%d" % (t, k), 6.0)
         pr = tile()
         mm([(ps(pr, j, SL * n, SL), [(A("I1"), w)]) for j in range(SL)])
         for q in range(15 // SL):
@@ -377,7 +376,6 @@ def build():
         ts(b("kj"), b("ki"), V - 1, ALU.bitwise_and)
         cp(b("ku"), b("kj"))
         cp2(m, ind(b("bz"), b("ku")))
-        send("next", [(cut("ML", t, k, 0, 1), m, 8, 0)], "ma%d_%d" % (t, k), 4.0)
         ts(sl("dd", k * C, k * C + C), b("ky", 15, 16 * C, 16), 0.5, ALU.is_ge, float(WR), ALU.mult)
         for q in range(16 // SG):
             pd = tile()
@@ -390,12 +388,11 @@ def build():
         ts(hp, y, 480.0, ALU.is_lt)
         tt(tri("SB", t, k, 1), y, b("ry"), ALU.is_ge)
         tt(tri("SB", t, k, 0), hp, tri("SB", t, k, 1), ALU.subtract)
-        send("next", [(cut("LB", t, k, None, 5), cut("SB", t, k, None, 5), 8, 1)], "mb%d_%d" % (t, k), 5.5)
 
     def writes(t):
         now[0] = None
         m = sl("MS", t * L, t * L + L)
-        z = A("zp") if t == 0 else sl("ML", (t - 1) * L, t * L)
+        z = A("zp") if t == 0 else sl("MS", (t - 1) * L, t * L)
         p6 = tile()
         u = ps(p6, L, L + 12)
         mj = [sl("MS", t * L + j, t * L + L, 16) for j in range(16)]
@@ -403,20 +400,15 @@ def build():
         mm([(ps(p7, 0, L), [(A("Ih"), m), (A("Ih"), z), (A("In"), A("ch")), (A("I1"), A("cM1")), (A("In"), A("cM1"))])])
         mm([(u, [(zk("Zn", j), mj[j]) for j in range(16)] + [(A("I1"), A("c15")), (A("I1"), sl("cM4", 0, 12)), (A("In"), sl("cM4", 0, 12))]
              + [(zk("Zu", j), mj[j]) for j in range(16)] + [(A("I1"), A("b4")), (A("I1"), A("dd"))])])
-        cp2(A("nv"), ps(p7, 0, L))
-        cp(A("uA"), u)
-        cp(ind(sl("X", 0, XR), A("uA")), A("nv"))
-        if t < RO - 1:
-            ts(A("d2"), A("dd"), -2.0, ALU.mult, float(WR), ALU.add)
-            tt(A("sB"), u, A("d2"), ALU.add)
-            cp(A("uB"), A("sB"))
+        cp2(sl("US", UW * t, UW * t + L), ps(p7, 0, L))
+        cp2(sl("US", UW * t + L, UW * t + UW), u)
 
     def phase_b(t, k):
         now[0] = k
 
         def b(nm, lo=None, hi=None, st=1):
             return A("%s%d" % (nm, k)) if lo is None else sl("%s%d" % (nm, k), lo, hi, st)
-        m = cut("ML", t, k, 0, 1)
+        m = cut("MS", t, k, 0, 1)
         p0 = tile()
         mm([(ps(p0, 0, n), [(A("I1"), A("cah")), (A("I1"), A("cal")), (A("Gh"), m), (A("Gl"), m), (A("I1"), A("cMv")), (A("In"), A("cMv")),
                             (A("Hh"), m), (A("Hl"), m)])])
@@ -424,43 +416,67 @@ def build():
         h = n // CSPLIT
         for j in range(CSPLIT):
             lo, hi = 16 * h * j, 16 * h * (j + 1)
-            cp2(b("cc", lo, hi), ind(sl("X", XR, XR + V), b("hu", h * j, h * j + h)))
+            cp2(b("cc", lo, hi), ind(sl("X%d" % (t + 1), WR, WR + V), b("hu", h * j, h * j + h)))
             scan(b("mx", lo, hi), sl("rmx", lo, hi), b("cc", lo, hi), ALU.min, ALU.max)
             scan(b("mn", lo, hi), sl("rmn", lo, hi), b("cc", lo, hi), ALU.max, ALU.min)
         p1 = tile()
         mm([(ps(p1, 0, n), [(A("In"), m), (A("In"), m), (A("I1"), b("mx", 15, 16 * n, 16)), (A("I1"), b("mn", 15, 16 * n, 16))])])
         act(b("gf"), ps(p1, 0, n), ACT.Sign, bias=-1.5)
         p2 = tile()
-        ap_ = cut("LB", t, k, 4, 5)
+        ap_ = cut("SB", t, k, 4, 5)
         mm([(ps(p2, 0, n), ([(A("In"), ap_)] if t > 0 else []) + [(A("B1"), b("gf"))])])
         ts(b("u3", 1, 3 * n, 3), ps(p2, 0, n), -0.5, ALU.is_ge)
-        scan(tri("SB", t + 1, k), b("u3"), tri("LB", t, k), ALU.mult, ALU.add)
+        scan(tri("SB", t + 1, k), b("u3"), tri("SB", t, k), ALU.mult, ALU.add)
         p3 = tile()
-        mm([(ps(p3, 0, n), [(A("In"), cut("LB", t, k, 3, 5)), (A("I1"), b("u3", 1, 3 * n, 3)), (A("I4"), tri("SB", t + 1, k, 1))])])
+        mm([(ps(p3, 0, n), [(A("In"), cut("SB", t, k, 3, 5)), (A("I1"), b("u3", 1, 3 * n, 3)), (A("I4"), tri("SB", t + 1, k, 1))])])
         ts(b("e2", 1, 2 * n, 2), ps(p3, 0, n), 4.0, ALU.is_equal)
-        scan(b("ah") if t < RO - 1 else duo("FW", 0, k), b("e2"), duo("LF", t, k), ALU.mult, ALU.add)
+        scan(b("ah") if t < RO - 1 else duo("FW", 0, k), b("e2"), duo("SF", t, k), ALU.mult, ALU.add)
 
+    def hand_on(c, also=()):
+        now[0] = None
+        for j in range(KP):
+            lo, hi = WR + j * V // KP, WR + (j + 1) * V // KP
+            send(-1, [(sl("X%d" % c, lo, hi), sl("X%d" % (c - 1), lo, hi), 8, 2 * (j % 2))], "k%d_%d" % (c, j), KLAT, j % 2 == 1, also)
+            ops[-1]["first"] = (0.3 if c < 3 else 0.15) - 0.04 * j
+            if c + j == 1:
+                ops[-1]["ways"]["G"] = (ops[-1]["ways"]["G"][0], 3.0)
+
+    def put(c, name, j):
+        now[0] = None
+        off = sl("uo", 16 * (j % 4), 16 * (j % 4) + 12)
+        cp(off, sl(name, UW * j + L, UW * j + L + 12))
+        cp(ind(sl("X%d" % c, 0, 2 * WR), off), sl(name, UW * j, UW * j + L))
+
+    hand_on(1)
+    hand_on(2)
+    slot = 0
     for t in range(RO):
         for k in range(NCH):
             phase_a(t, k)
         writes(t)
+        holders = [c for c in range(RO + 1) if c == 0 or (c > t and t < RO - 1)]
+        came = []
+        for c in sorted(holders, key=lambda c_: (c_ == 0, c_)):
+            if c == t:
+                came.append((c, "US", t))
+                continue
+            send(t - c, [(sl("UL", UW * slot, UW * slot + UW), sl("US", UW * t, UW * t + UW), 8, 3 if c > t + 1 else 1)], "u%d" % slot, ULAT, c > t + 1)
+            came.append((c, "UL", slot))
+            slot += 1
+        if t == 0:
+            hand_on(3, [sl("US", 0, UW)])
         for k in range(NCH):
             phase_b(t, k)
-        now[0] = None
-        if t < RO - 1:
-            cp(ind(sl("X", XB, XD + WR), A("uB")), A("nv"))
-    dma("Y", ext("xn", 0, WR), sl("X", XA, XR), "stx", 2.5)
-    send("home", [(A("GL"), sl("ML", (RO - 1) * L, RO * L), 8, 1)], "finz", 5.0)
-    dma("Y", ext("zn", 0, L), A("GL"), "stz", 2.0)
+        for c, name, j in came:
+            put(c, name, j)
+    dma("Y", ext("xn", 0, WR), sl("X0", WR, 2 * WR), "stx", 2.5)
+    dma("Y", ext("zn", 0, L), sl("MS", (RO - 1) * L, RO * L), "stz", 2.0)
     for k in range(NCH):
         now[0] = k
         cp2(cut("FS", 0, k, 1), tri("SB", RO, k, 2))
         lin2(cut("FS", 0, k, 0), duo("FW", 0, k, 1), 1.0, 2048.0)
-        send("home", [(cut("FL", 0, k, j), cut("FS", 0, k, j), 4, 2 * j) for j in range(2)], "fin%d" % k, 4.5)
-    for k in range(NCH):
-        now[0] = k
-        dma("Y", ext("wn", k * n, k * n + n), cut("FL", 0, k, 0), "sw%d" % k, 2.0)
-        dma("Y" if k < NCH - 1 else "S", ext("dn", k * n, k * n + n), cut("FL", 0, k, 1), "sd%d" % k, 2.0)
+        dma("Y", ext("wn", k * n, k * n + n), cut("FS", 0, k, 0), "sw%d" % k, 2.0)
+        dma("Y", ext("dn", k * n, k * n + n), cut("FS", 0, k, 1), "sd%d" % k, 2.0)
     byname, bytile = {}, {}
     for i, o in enumerate(ops):
         deps = set()
@@ -497,7 +513,7 @@ def schedule(ops, bytile, win, stag, lift, vpen):
     rank = [0.0] * N_
     for i in range(N_ - 1, -1, -1):
         rank[i] = min(w[1] for w in ops[i]["ways"].values()) + ops[i]["lat"] + max([LAT + rank[j] for j in succ[i]] + [0.0])
-        rank[i] += 100.0 if ops[i].get("first") else 0.0
+        rank[i] += 100.0 * ops[i].get("first", 0)
     prio = [rank[i] - stag * (ops[i]["tag"] or 0) + lift[i] for i in range(N_)]
     free = {e: 0.0 for e in "VSPGY"}
     end, order, at = {}, [], {}
@@ -585,13 +601,15 @@ def plan(win, stag, pen, rounds, seed):
                     continue
                 if p["eng"] not in need or pos[j] > pos[need[p["eng"]]]:
                     need[p["eng"]] = j
-            else:
+            elif hits(o["R"] + o["W"], p["W"]) or p["calls"][0][0] != "send":
                 need[p["sem"]] = j
+            else:
+                need["left_" + p["sem"]] = j
         o["need"] = []
         for key, j in sorted(need.items()):
             if pos[j] > last.get((o["eng"], key), -1):
                 last[(o["eng"], key)] = pos[j]
-                o["need"].append(j)
+                o["need"].append((j, key if key.startswith("left_") else None))
                 ops[j]["inc"] = True
     cnt = {}
     for i in order:
@@ -604,7 +622,7 @@ def plan(win, stag, pen, rounds, seed):
     return ops, order, bank, total
 
 
-PLAN = plan(0.08, 2.0, 1.0, 1500, 0)
+PLAN = plan(0.08, 1.0, 0.8, 1800, 0)
 
 
 def helpers(topo, src, dst):
@@ -614,7 +632,7 @@ def helpers(topo, src, dst):
 
 def route(T, topo, r, kind, which):
     src = T.cores[r]
-    dst = T.cores[(r - RO) % NR] if kind == "home" else T.cores[(r + 1) % NR]
+    dst = T.cores[(r + kind) % NR]
     return dst, (dst if topo.may_write(src, dst) else helpers(topo, src, dst)[which])
 
 
@@ -634,19 +652,18 @@ def rank_program(g, core, T, topo):
             return T[pool][:, at + lo:at + hi:st] if st != 1 else T[pool][:, at + lo:at + hi]
         return T[ap[1].replace("wsx", "wsg")][(slice(None),) + tuple(slice(x.start, x.stop) if isinstance(x, slice) and x.step == 1 else x for x in ap[2])]
 
+    left = []
+
     def write(parts, sem, high):
-        tr, used = [], 0
-        for to, d_, s_, ne in parts:
-            eng = topo.engines(core, to)
-            eng = eng[::-1] if high else eng
-            tr.append((topo.addr(to, core), sum(1 << e for e in eng[used:used + ne]), res(d_), res(s_)))
-            used += ne
-        if len(tr) == 1:
-            g.remote_dma(tr[0][2], tr[0][3], T.sem[sem], T.sem.sent, tr[0][0][1], tr[0][0][0], tr[0][1])
-        else:
-            g.remote_dma_fused([RemoteDMATransfer(dst_ids=[DstId(rid=a_[0], pnc=a_[1])], dma_engine_mask=mk, remote_sem=T.sem[sem], src=s_, dst=d_)
-                                for a_, mk, d_, s_ in tr], local_sem=T.sem.sent)
-        return used
+        (to, d_, s_, ne), = parts
+        eng = topo.engines(core, to)
+        eng = eng[::-1] if high else eng
+        rid, pid = topo.addr(to, core)
+        own = "left_" + sem in SEMAPHORES
+        g.remote_dma(res(d_), res(s_), T.sem[sem], T.sem["left_" + sem if own else "sent"], pid, rid, sum(1 << e for e in eng[:ne]))
+        if own:
+            left.append(("left_" + sem, ne))
+        return 0 if own else ne
 
     rank = T.rank_of(core)
     sent = 0
@@ -660,8 +677,8 @@ def rank_program(g, core, T, topo):
                 if mine:
                     g.wait_ge(T.sem[args[2]], sum(p[3] for p in mine))
                     sent += write(mine, args[2], False)
-        if sent:
-            g.wait_ge(T.sem.sent, sent)
+        for s_, v in left + ([("sent", sent)] if sent else []):
+            g.wait_ge(T.sem[s_], v)
         return
     Q = {"V": g.vector, "S": g.scalar, "P": g.tensor, "G": g, "Y": g.sync}
     call = {
@@ -672,8 +689,8 @@ def rank_program(g, core, T, topo):
     for i in order:
         o = ops[i]
         q = Q[o["eng"]]
-        for j in o["need"]:
-            q.wait_ge(T.sem[ops[j]["sig"][0]], ops[j]["sig"][1])
+        for j, key in o["need"]:
+            q.wait_ge(T.sem[key or ops[j]["sig"][0]], ops[j]["sig"][1])
         ins = None
         for name, args, kw in o["calls"]:
             if name == "send":
@@ -686,6 +703,5 @@ def rank_program(g, core, T, topo):
                 ins = call[name](*[res(x) for x in args], **kw)
         if ins is not None and o["inc"]:
             ins.then_inc(T.sem[o["sig"][0]], 1)
-    g.wait_ge(T.sem.sent, sent)
-    for s_ in tail:
-        g.wait_ge(T.sem[s_], 16)
+    for s_, v in left + [("sent", sent)] + [(s_, 16) for s_ in tail]:
+        g.wait_ge(T.sem[s_], v)

import math
import numpy as np
from concourse.mybir import AluOpType as ALU
from concourse.mybir import ActivationFunctionType as ACT

V, L, D, RO, NR = 4096, 192, 5, 3, 8
NCH = 3
n = L // NCH
C = n // 16
SL, SG = 5, 8
WR = 4 * L
KP, UW = 4, L + 12
KLAT, ULAT = 9.0, 5.5
M1, M2, M4, M64 = 1.5 * 2 ** 23, 1.5 * 2 ** 24, 1.5 * 2 ** 25, 1.5 * 2 ** 29
HUGE = float(2 ** 23)
CSPLIT, BSPLIT = 2, 2
F16 = "float16"

SCRATCH = {}
BUF = {}
HOME = {}


def _sb(name, cols, dtype):
    BUF[name] = ("sbuf", [128] + (list(cols) if isinstance(cols, (list, tuple)) else [cols]), dtype)
    if isinstance(cols, int) and cols <= 200:
        pool = "pool_" + dtype
        at = SCRATCH[pool][1][1] if pool in SCRATCH else 0
        HOME[name] = (pool, at)
        SCRATCH[pool] = ("sbuf", [128, at + (cols + 15) // 16 * 16], dtype)
    else:
        SCRATCH[name] = BUF[name]


BF, F32, I32, U16 = "bfloat16", "float32", "int32", "uint16"
for _k in range(RO + 1):
    _sb("X%d" % _k, WR + V, BF)
for _nm, _c, _d in (
        ("nti", 8, I32), ("ntf", 8, F32), ("wi", L, I32), ("di", L, I32), ("df", L, F32), ("zp", L, BF),
        ("pi", 4, I32), ("pj", 4, I32), ("col", 8, F32), ("xi", 144, I32), ("xj", 128, I32), ("cw", 144, BF),
        ("Pf", 5 * 128, F16), ("PI", 5 * 128, BF), ("PD", 4 * 128, BF), ("If", 128, F16), ("Ie", 128, F16),
        ("I1", 128, BF), ("Id", 128, BF), ("I4", 128, BF), ("In", 128, BF), ("Ih", 128, BF),
        ("B1", 128, BF), ("Y", 128, BF), ("MK", 16 * 128, BF), ("s1", 16, F32), ("s2", 16, F32),
        ("Z1", 144, BF), ("Z65", 144, BF), ("Zu", 144, BF), ("Hf", 128, F32), ("Hg", 128, F32), ("Hh", 128, BF), ("Hl", 128, BF),
        ("dl5", 5 * n, F32), ("dl16", 16 * C, F32), ("rmx", 16 * n, BF), ("rmn", 16 * n, BF),
        ("ch", L, BF), ("c8", n, BF), ("b16", C, F32), ("b4", 12, BF), ("c2k", n, BF), ("cM1", L, BF), ("cM2", n, BF), ("cM4", n, BF),
        ("c15", 12, BF), ("Bn", 128, BF), ("Zn", 144, BF),
        ("SB", 4 * 5 * L, BF), ("SF", 3 * 2 * L, F32), ("MS", 3 * L, BF), ("FW", 2 * L, F32), ("FS", 2 * L, F32),
        ("US", 3 * UW, F32), ("UL", 7 * UW, F32), ("uo", 64, U16),
        ("Gh", 128, BF), ("Gl", 128, BF), ("cf", n, F32), ("cah", n, BF), ("cal", n, BF), ("cMv", n, BF),
        ("dd", 12, BF)):
    _sb(_nm, _c, _d)
for _k in range(NCH):
    for _nm, _c, _d in (
            ("fq", n, BF), ("T5", 5 * n, F32), ("ina", n, BF), ("x", n, F32), ("yi", n, I32), ("ixi", n, I32), ("ixu", n, U16),
            ("bz", 32 * n, BF), ("shi", n, BF), ("slo", n, BF), ("sg", 15 * n, BF), ("wsg", [n, 16], BF),
            ("sa", 16 * C, BF), ("ky", 16 * C, F32), ("ki", C, I32), ("kj", C, I32), ("ku", C, U16), ("sgm", 16 * n, BF), ("ry", n, F32),
            ("hu", n, U16), ("cc", 16 * n, BF), ("mx", 16 * n, BF), ("mn", 16 * n, BF),
            ("gf", n, BF), ("u3", 3 * n, BF), ("e2", 2 * n, BF), ("ah", 2 * n, F16)):
        _sb("%s%d" % (_nm, _k), _c, _d)
    BUF["wsx%d" % _k] = BUF["wsg%d" % _k]
for _k in range(8):
    SCRATCH["pb%d" % _k] = ("psum", [128, 512], F32)

SEMAPHORES = ["sV", "sS", "sP", "sG", "sent", "ld0", "ld1", "ld2", "ld3", "stx", "stz"] + ["u%d" % _k for _k in range(7)]
for _k in range(NCH):
    SEMAPHORES += ["sw%d" % _k, "sd%d" % _k]
for _k in range(KP):
    SEMAPHORES += ["lx%d" % _k] + ["k%d_%d" % (_c, _k) for _c in (1, 2, 3)] + ["left_k%d_%d" % (_c, _k) for _c in (1, 2, 3)]

CY, CP, FIX, LAT, ISSUE = 0.00095, 0.00048, 0.06, 0.10, 1.0
BYTES = {BF: 2, F32: 4, I32: 4, U16: 2, "float16": 2}


def A(name, *ix):
    return ("s", name, ix if ix else (slice(None),))


def sl(name, lo, hi, st=1):
    return ("s", name, (slice(lo, hi, st),))


def ps(tile, lo, hi, st=1):
    return ("p", tile, (slice(lo, hi, st),))


def ind(win, off):
    return ("i", win, off)


def ext(name, lo, hi):
    return ("x", name, (slice(lo, hi),))


def span(ap):
    shape = BUF[ap[1]][1][1:]
    a = np.arange(int(np.prod(shape))).reshape(shape)[ap[2]]
    return int(a.min()), int(a.max()) + 1, int(a.size)


def count(ap):
    if ap[0] == "i":
        return 16 * span(ap[2])[2]
    if ap[0] == "p":
        return len(range(512)[ap[2][0]])
    return span(ap)[2]


def two(ap):
    return ap[0] == "s" and BYTES[BUF[ap[1]][2]] == 2


def build():
    ops = []
    tiles, now = [0], [None]
    ALL = slice(None)

    def tile():
        tiles[0] += 1
        return tiles[0]

    def add(ways, outs, ins, sem=None, lat=0.0, val=16):
        R, W, P = [], [], set()
        for lst, aps in ((W, outs), (R, ins)):
            for ap in aps:
                if not isinstance(ap, tuple):
                    continue
                if ap[0] == "i":
                    lst.append((ap[1][1],) + span(ap[1])[:2])
                    R.append((ap[2][1],) + span(ap[2])[:2])
                elif ap[0] == "p":
                    P.add(ap[1])
                elif ap[0] == "s":
                    lst.append((ap[1],) + span(ap)[:2])
        ops.append({"ways": ways, "R": R, "W": W, "P": P, "sem": sem, "lat": lat, "val": val, "tag": now[0],
                    "PW": set(ap[1] for ap in outs if isinstance(ap, tuple) and ap[0] == "p")})

    def vcost(out, ins, per):
        k = count(out)
        if out[0] == "i":
            return FIX + 3.5 * k * CY
        if ins and ins[0][0] == "i":
            return FIX + 1.56 * k * CY
        return FIX + max(64 * CY - FIX, 0, per * k * CY)

    def half(aps):
        return 0.5 if all(two(a) for a in aps) else 1.0

    def w_ts(out, a, s1, op0, s2=None, op1=None):
        args = (out, a, s1, s2, op0) + ((op1,) if op1 is not None else ())
        return [("tensor_scalar", args, {})], vcost(out, [a], half([out, a]))

    def w_act(out, a, f, bias=None, scale=None):
        kw = {}
        if bias is not None:
            kw["bias"] = bias
        if scale is not None:
            kw["scale"] = scale
        return [("activation", (out, a, f), kw)], vcost(out, [a], 1.0)

    def w_cp(out, a):
        return [("tensor_copy", (out, a), {})], vcost(out, [a], half([out, a]))

    def ts(out, a, s1, op0, s2=None, op1=None):
        add({"V": w_ts(out, a, s1, op0, s2, op1)}, [out], [a, s1, s2])

    def tt(out, a, b, op):
        add({"V": ([("tensor_tensor", (out, a, b, op), {})], vcost(out, [a], 1.0 if "p" in (a[0], b[0]) else 2.0))}, [out], [a, b])

    def cp(out, a):
        add({"V": w_cp(out, a)}, [out], [a])

    def ms(out, v):
        add({"V": ([("memset", (out, v), {})], vcost(out, [], half([out])))}, [out], [])

    def scan(out, d0, d1, op0, op1):
        add({"V": ([("tensor_tensor_scan", (out, d0, d1, 0.0, op0, op1), {})], vcost(out, [d0], half([out, d0, d1])))}, [out], [d0, d1])

    def act(out, a, f, bias=None, scale=None):
        add({"S": w_act(out, a, f, bias, scale)}, [out], [a])

    def cp2(out, a):
        add({"S": w_act(out, a, ACT.Copy), "V": w_cp(out, a)}, [out], [a])

    def lin2(out, a, mul, plus):
        add({"S": w_act(out, a, ACT.Identity if plus else ACT.Copy, plus if plus else None, mul if mul != 1.0 else None),
             "V": w_ts(out, a, mul, ALU.mult, plus, ALU.add)}, [out], [a])

    def sign2(out, a):
        add({"S": w_act(out, a, ACT.Sign), "V": w_ts(out, a, 1.0, ALU.min, -1.0, ALU.max)}, [out], [a])

    def mm(groups, also=()):
        calls, outs, ins, cost = [], [], list(also), 0.03
        for out, terms in groups:
            outs.append(out)
            for j, (l, r) in enumerate(terms):
                calls.append(("matmul", (out, l, r, j == 0, j == len(terms) - 1), {}))
                ins += [l, r]
                cost += max(64, count(r)) * CP * (1 if two(r) else 4)
        add({"P": (calls, cost)}, outs, ins)

    def iota(out, pat, base, cm):
        kw = {} if BUF[out[1]][2] == I32 else {"allow_small_or_imprecise_dtypes": True}
        add({"G": ([("iota", (out, pat, base, cm), kw)], 0.13 + 2 * count(out) * CY)}, [out], [])

    def dma(eng, out, a, sem, lat):
        add({eng: ([("dma_start", (out, a), {})], 0.1 if eng != "G" else 1.0)}, [out], [a], sem=sem, lat=lat)

    def send(kind, parts, sem, lat, high=False, also=()):
        add({"G": ([("send", (kind, parts, sem, high), {})], ISSUE)}, [p[0] for p in parts], [p[1] for p in parts] + list(also),
            sem=sem, lat=lat, val=sum(p[2] for p in parts))

    def blk(name, j):
        return sl(name, 128 * j, 128 * j + 128)

    def zk(name, k):
        return sl(name, 15 - k, 143 - k)

    def tri(name, t, k, j=None):
        o = (t * NCH + k) * 5 * n
        return sl(name, o, o + 3 * n) if j is None else sl(name, o + j, o + 3 * n, 3)

    def duo(name, t, k, j=None):
        o = (t * NCH + k) * 2 * n
        return sl(name, o, o + 2 * n) if j is None else sl(name, o + j, o + 2 * n, 2)

    def cut(name, t, k, j, parts=2):
        o = (t * NCH + k) * parts * n
        return sl(name, o, o + parts * n) if j is None else sl(name, o + j * n, o + j * n + n)

    for j, (eng, out, src, lat) in enumerate((("Y", sl("nti", 0, D), ext("nt", 0, D), 2.2), ("S", A("di"), ext("d0", 0, L), 2.2),
                                              ("Y", A("wi"), ext("w0", 0, L), 2.2))):
        dma(eng, out, src, "ld%d" % j, lat)
        ops[-1]["first"] = 9 - j
    for j in range(KP):
        dma("Y", sl("X0", WR + j * V // KP, WR + (j + 1) * V // KP), ext("xs", j * V // KP, (j + 1) * V // KP), "lx%d" % j, 2.5 + 4.0 * (j + 1) / KP)
        ops[-1]["first"] = 5 - j
    dma("Y", A("zp"), ext("z0", 0, L), "ld3", 7.0)
    iota(sl("pi", 0, 1), [[0, 1]], 0, 1)
    iota(A("xi"), [[1, 144]], 0, 0)
    iota(A("dl5"), [[0, n], [-16384, 5]], 8192, 0)
    ms(sl("dl5", 0, 5 * n, 5), HUGE)
    for k in range(NCH):
        for j in range(4):
            iota(sl("bz%d" % k, 4 * n * j, 4 * n * (j + 1)), [[0, 4 * n]], 0, 0)
    for j in range(4):
        iota(sl("rmx", 4 * n * j, 4 * n * (j + 1)), [[0, n // 4], [2048, 16]], -1024, 0)
        iota(sl("rmn", 4 * n * j, 4 * n * (j + 1)), [[0, n // 4], [-2048, 16]], 1024, 0)
    g16, kc, c1, c2, c3, c16, c4 = (sl("col", j, j + 1) for j in range(7))
    ts(sl("pj", 0, 1), sl("pi", 0, 1), 112, ALU.bitwise_and)
    ts(sl("pj", 1, 2), sl("pi", 0, 1), 15, ALU.bitwise_and)
    cp(sl("col", 0, 2), sl("pj", 0, 2))
    ts(A("cw"), A("xi"), g16, ALU.subtract)
    cm = sl("cw", 0, 128)
    cp(sl("ntf", 0, D), sl("nti", 0, D))
    ts(A("I1"), cm, kc, ALU.is_equal)
    ts(A("Ie"), cm, kc, ALU.is_equal)
    ts(A("If"), cm, kc, ALU.is_equal, 2080.0, ALU.mult)
    for e in range(D):
        ts(blk("Pf", e), cm, sl("ntf", e, e + 1), ALU.is_equal)
    for es in ((0, 1, 2), (3, 4)):
        pc = tile()
        mm([(ps(pc, 128 * j, 128 * j + 128), [(blk("Pf", e), A("Ie")), (A("I1"), A("I1"))]) for j, e in enumerate(es)])
        cp2(sl("PI", 128 * es[0], 128 * es[-1] + 128), ps(pc, 0, 128 * len(es)))
        for j, e in enumerate(es):
            if e < 4:
                lin2(blk("PD", e), blk("PI", e), 8192.0 * (4 - e), 0.0)
    lin2(A("Id"), A("I1"), 2464.0, 0.0)
    lin2(A("I4"), A("I1"), 4.0, 0.0)
    lin2(A("In"), A("I1"), -1.0, 0.0)
    lin2(A("Ih"), A("I1"), 0.5, 0.0)
    ts(A("xj"), sl("xi", 0, 128), 112, ALU.bitwise_and)
    ts(A("B1"), A("xj"), g16, ALU.is_equal)
    ts(A("Z1"), A("cw"), 15.0, ALU.is_equal)
    lin2(A("Z65"), A("Z1"), 65.0, 0.0)
    lin2(c1, kc, 4.0, 3.0)
    lin2(c2, kc, 2.0, 1.0)
    lin2(c3, kc, 333.0, 0.0)
    lin2(c16, kc, 16.0, 0.0)
    lin2(c4, kc, 4.0, 0.0)
    ts(A("Zu"), A("Z1"), c2, ALU.mult)
    pc = tile()
    mm([(ps(pc, 0, 128), [(A("I1"), A("I1")), (A("I1"), A("I1")), (A("In"), A("B1"))])])
    cp2(A("Y"), ps(pc, 0, 128))
    ts(A("s1"), sl("xi", 0, 16), kc, ALU.is_equal, -1.0, ALU.mult)
    ts(A("s2"), sl("xi", 0, 16), kc, ALU.not_equal)
    for k in range(15):
        ts(blk("MK", k), A("Y"), sl("s1", k, k + 1), ALU.max, sl("s2", k, k + 1), ALU.min)
    ts(A("Hf"), cm, c1, ALU.mult, c2, ALU.add)
    tt(A("Hg"), A("Hf"), A("B1"), ALU.mult)
    cp2(A("Hh"), A("Hg"))
    tt(A("Hl"), A("Hg"), A("Hh"), ALU.subtract)
    ms(A("dl16"), 1.0)
    ms(sl("dl16", 0, 16 * C, 16), HUGE)
    ms(sl("dl16", 15, 16 * C, 16), float(16 * n))
    for nm, v in (("c8", -8.5), ("c2k", 2080.0), ("cM1", M1), ("cM2", M2), ("cM4", M4), ("c15", 1.5)):
        ms(A(nm), v)
    act(A("ch"), A("cM1"), ACT.Sigmoid, bias=-math.log(3.0), scale=0.0)
    ops[-1]["ways"]["S"] = (ops[-1]["ways"]["S"][0], ops[-1]["ways"]["S"][1] + 1.5)
    ops[-1]["first"] = True
    lin2(A("Bn"), A("B1"), -1.0, 0.0)
    lin2(A("Zn"), A("Zu"), -1.0, 0.0)
    lin2(A("Gh"), A("Hh"), -1.0, 0.0)
    lin2(A("Gl"), A("Hl"), -1.0, 0.0)
    ms(A("cMv"), V * M1)
    ts(A("cf"), A("ch", slice(0, n)), 8190.0, ALU.mult, c3, ALU.subtract)
    cp2(A("cah"), A("cf"))
    tt(A("cal"), A("cf"), A("cah"), ALU.subtract)
    ts(A("b16"), sl("xi", 0, C), 256.0, ALU.mult, c16, ALU.add)
    ts(A("b4"), sl("xi", 0, L // 16), 64.0, ALU.mult, c4, ALU.add)
    for k in range(NCH):
        ms(A("u3%d" % k), 1.0)
        ms(sl("u3%d" % k, 0, 3 * n, 3), 0.0)
        ms(A("e2%d" % k), 0.0)
    cp(A("df"), A("di"))
    for k in range(NCH):
        now[0] = k
        cp2(tri("SB", 0, k, 2), sl("df", k * n, k * n + n))
        ts(sl("ah%d" % k, 1, 2 * n, 2), sl("wi", k * n, k * n + n), -2048.0, ALU.add)

    def phase_a(t, k):
        now[0] = k

        def b(nm, lo=None, hi=None, st=1):
            return A("%s%d" % (nm, k)) if lo is None else sl("%s%d" % (nm, k), lo, hi, st)
        d, ah, a = tri("SB", t, k, 2), b("ah", 1, 2 * n, 2), duo("SF", t, k, 1)
        z = sl("zp", k * n, k * n + n) if t == 0 else cut("MS", t - 1, k, 0, 1)
        m = cut("MS", t, k, 0, 1)
        act(b("fq"), d, ACT.Square, bias=-256.0, scale=64.0)
        p0, p2 = tile(), tile()
        mm([(ps(p0, e, 5 * n, 5), [(blk("Pf", e), ah)] + ([(blk("PD", e), d)] if e < 4 else []) + [(blk("PI", e), b("fq"))]) for e in range(D)])
        mm([(ps(p2, 0, n), [(A("If"), ah), (A("Id"), d)]), (ps(p2, n, 2 * n), [(A("Ie"), ah), (A("I1"), A("c2k"))]), (ps(p2, 2 * n, 3 * n), [(A("Ie"), ah)])])
        cp2(a, ps(p2, 2 * n, 3 * n))
        scan(b("T5"), A("dl5"), ps(p0, 0, 5 * n), ALU.add, ALU.min)
        Tp = b("T5", 4, 5 * n, 5)
        tt(b("x"), ps(p2, n, 2 * n), Tp, ALU.mult)
        tt(b("yi"), ps(p2, 0, n), b("x"), ALU.add)
        tt(duo("SF", t, k, 0), Tp, ps(p2, 2 * n, 3 * n), ALU.subtract)
        ts(b("ina"), Tp, 2048.0, ALU.is_ge, 4080.0, ALU.mult)
        ts(b("ixi"), b("yi"), 5, ALU.arith_shift_right, V - 1, ALU.bitwise_and)
        cp(b("ixu"), b("ixi"))
        h = n // BSPLIT
        for j in range(BSPLIT):
            cp2(b("bz", 16 * n + 16 * h * j, 16 * n + 16 * h * (j + 1)), ind(sl("X%d" % t, WR, WR + V), b("ixu", h * j, h * j + h)))
        cp2(b("bz", 0, 16 * n, 16), z)
        pw = tile()
        w = A("wsg%d" % k, ALL, 15)
        mm([(ps(pw, 0, n), [(A("I1"), d), (A("I1"), b("ina"))])])
        act(w, ps(pw, 0, n), ACT.Sigmoid, bias=-30.0 * math.log(2.0), scale=-math.log(2.0))
        if t > 0:
            pa = tile()
            hit = tri("SB", t, k, 1)
            mm([(ps(pa, 0, n), [(A("B1"), hit), (A("I1"), A("cM4")), (A("In"), A("cM4")), (A("Bn"), hit)])])
            act(cut("SB", t, k, 4, 5), ps(pa, 0, n), ACT.Abs)
        p3 = tile()
        s = ps(p3, 0, n)
        mm([(s, [(A("I4"), b("ina"))] + [(zk("Z1", j), b("bz", 16 * n + j, 32 * n, 16)) for j in range(16)])])
        cp2(b("shi"), s)
        tt(b("slo"), s, b("shi"), ALU.subtract)
        po = tile()
        mm([(ps(po, 0, n), [(A("I1"), b("shi")), (A("I1"), b("slo")), (A("I1"), A("cM2")), (A("In"), A("cM2")), (A("In"), b("shi")), (A("In"), b("slo"))])])
        act(cut("SB", t, k, 3, 5), ps(po, 0, n), ACT.Abs)
        pr = tile()
        mm([(ps(pr, j, SL * n, SL), [(A("I1"), w)]) for j in range(SL)])
        for q in range(15 // SL):
            pd = tile()
            sg = b("sg", q * SL * n, (q + 1) * SL * n)
            mm([(ps(pd, j, SL * n, SL), [(blk("MK", 14 - q * SL - j), b("shi")), (blk("MK", 14 - q * SL - j), b("slo"))]) for j in range(SL)])
            sign2(sg, ps(pd, 0, SL * n))
            tt(A("wsx%d" % k, ALL, slice(q * SL, q * SL + SL)), ps(pr, 0, SL * n), sg, ALU.mult)
        p4 = tile()
        mm([(ps(p4, 0, 16 * C), [(zk("Z1", j), A("wsg%d" % k, slice(j, n, 16), ALL)) for j in range(16)])], [A("wsx%d" % k)])
        act(b("sa"), ps(p4, 0, 16 * C), ACT.Abs, scale=float(2 ** 45))
        scan(b("ky"), A("dl16"), b("sa"), ALU.add, ALU.min)
        tt(b("ki"), b("ky", 15, 16 * C, 16), A("b16"), ALU.add)
        ts(b("kj"), b("ki"), V - 1, ALU.bitwise_and)
        cp(b("ku"), b("kj"))
        cp2(m, ind(b("bz"), b("ku")))
        ts(sl("dd", k * C, k * C + C), b("ky", 15, 16 * C, 16), 0.5, ALU.is_ge, float(WR), ALU.mult)
        for q in range(16 // SG):
            pd = tile()
            mm([(ps(pd, j * n, j * n + n), [(A("I1"), b("bz", 16 * n + q * SG + j, 32 * n, 16)), (A("In"), m)]) for j in range(SG)])
            act(b("sgm", q * SG * n, (q + 1) * SG * n), ps(pd, 0, SG * n), ACT.Sigmoid, bias=-math.log(64.0), scale=40.0)
        p5 = tile()
        y, hp = ps(p5, 0, n), ps(p5, n, 2 * n)
        mm([(y, [(A("I1"), b("ina")), (A("I1"), A("c8"))] + [(zk("Z65", j), b("sgm", j * n, j * n + n)) for j in range(16)])])
        ts(b("ry"), y, M64, ALU.add, M64, ALU.subtract)
        ts(hp, y, 480.0, ALU.is_lt)
        tt(tri("SB", t, k, 1), y, b("ry"), ALU.is_ge)
        tt(tri("SB", t, k, 0), hp, tri("SB", t, k, 1), ALU.subtract)

    def writes(t):
        now[0] = None
        m = sl("MS", t * L, t * L + L)
        z = A("zp") if t == 0 else sl("MS", (t - 1) * L, t * L)
        p6 = tile()
        u = ps(p6, L, L + 12)
        mj = [sl("MS", t * L + j, t * L + L, 16) for j in range(16)]
        p7 = tile()
        mm([(ps(p7, 0, L), [(A("Ih"), m), (A("Ih"), z), (A("In"), A("ch")), (A("I1"), A("cM1")), (A("In"), A("cM1"))])])
        mm([(u, [(zk("Zn", j), mj[j]) for j in range(16)] + [(A("I1"), A("c15")), (A("I1"), sl("cM4", 0, 12)), (A("In"), sl("cM4", 0, 12))]
             + [(zk("Zu", j), mj[j]) for j in range(16)] + [(A("I1"), A("b4")), (A("I1"), A("dd"))])])
        cp2(sl("US", UW * t, UW * t + L), ps(p7, 0, L))
        cp2(sl("US", UW * t + L, UW * t + UW), u)

    def phase_b(t, k):
        now[0] = k

        def b(nm, lo=None, hi=None, st=1):
            return A("%s%d" % (nm, k)) if lo is None else sl("%s%d" % (nm, k), lo, hi, st)
        m = cut("MS", t, k, 0, 1)
        p0 = tile()
        mm([(ps(p0, 0, n), [(A("I1"), A("cah")), (A("I1"), A("cal")), (A("Gh"), m), (A("Gl"), m), (A("I1"), A("cMv")), (A("In"), A("cMv")),
                            (A("Hh"), m), (A("Hl"), m)])])
        ts(b("hu"), ps(p0, 0, n), c3, ALU.add)
        h = n // CSPLIT
        for j in range(CSPLIT):
            lo, hi = 16 * h * j, 16 * h * (j + 1)
            cp2(b("cc", lo, hi), ind(sl("X%d" % (t + 1), WR, WR + V), b("hu", h * j, h * j + h)))
            scan(b("mx", lo, hi), sl("rmx", lo, hi), b("cc", lo, hi), ALU.min, ALU.max)
            scan(b("mn", lo, hi), sl("rmn", lo, hi), b("cc", lo, hi), ALU.max, ALU.min)
        p1 = tile()
        mm([(ps(p1, 0, n), [(A("In"), m), (A("In"), m), (A("I1"), b("mx", 15, 16 * n, 16)), (A("I1"), b("mn", 15, 16 * n, 16))])])
        act(b("gf"), ps(p1, 0, n), ACT.Sign, bias=-1.5)
        p2 = tile()
        ap_ = cut("SB", t, k, 4, 5)
        mm([(ps(p2, 0, n), ([(A("In"), ap_)] if t > 0 else []) + [(A("B1"), b("gf"))])])
        ts(b("u3", 1, 3 * n, 3), ps(p2, 0, n), -0.5, ALU.is_ge)
        scan(tri("SB", t + 1, k), b("u3"), tri("SB", t, k), ALU.mult, ALU.add)
        p3 = tile()
        mm([(ps(p3, 0, n), [(A("In"), cut("SB", t, k, 3, 5)), (A("I1"), b("u3", 1, 3 * n, 3)), (A("I4"), tri("SB", t + 1, k, 1))])])
        ts(b("e2", 1, 2 * n, 2), ps(p3, 0, n), 4.0, ALU.is_equal)
        scan(b("ah") if t < RO - 1 else duo("FW", 0, k), b("e2"), duo("SF", t, k), ALU.mult, ALU.add)

    def hand_on(c, also=()):
        now[0] = None
        for j in range(KP):
            lo, hi = WR + j * V // KP, WR + (j + 1) * V // KP
            send(-1, [(sl("X%d" % c, lo, hi), sl("X%d" % (c - 1), lo, hi), 8, 2 * (j % 2))], "k%d_%d" % (c, j), KLAT, j % 2 == 1, also)
            ops[-1]["first"] = (0.3 if c < 3 else 0.15) - 0.04 * j
            if c + j == 1:
                ops[-1]["ways"]["G"] = (ops[-1]["ways"]["G"][0], 3.0)

    def put(c, name, j):
        now[0] = None
        off = sl("uo", 16 * (j % 4), 16 * (j % 4) + 12)
        cp(off, sl(name, UW * j + L, UW * j + L + 12))
        cp(ind(sl("X%d" % c, 0, 2 * WR), off), sl(name, UW * j, UW * j + L))

    hand_on(1)
    hand_on(2)
    slot = 0
    for t in range(RO):
        for k in range(NCH):
            phase_a(t, k)
        writes(t)
        holders = [c for c in range(RO + 1) if c == 0 or (c > t and t < RO - 1)]
        came = []
        for c in sorted(holders, key=lambda c_: (c_ == 0, c_)):
            if c == t:
                came.append((c, "US", t))
                continue
            send(t - c, [(sl("UL", UW * slot, UW * slot + UW), sl("US", UW * t, UW * t + UW), 8, 3 if c > t + 1 else 1)], "u%d" % slot, ULAT, c > t + 1)
            came.append((c, "UL", slot))
            slot += 1
        if t == 0:
            hand_on(3, [sl("US", 0, UW)])
        for k in range(NCH):
            phase_b(t, k)
        for c, name, j in came:
            put(c, name, j)
    dma("Y", ext("xn", 0, WR), sl("X0", WR, 2 * WR), "stx", 2.5)
    dma("Y", ext("zn", 0, L), sl("MS", (RO - 1) * L, RO * L), "stz", 2.0)
    for k in range(NCH):
        now[0] = k
        cp2(cut("FS", 0, k, 1), tri("SB", RO, k, 2))
        lin2(cut("FS", 0, k, 0), duo("FW", 0, k, 1), 1.0, 2048.0)
        dma("Y", ext("wn", k * n, k * n + n), cut("FS", 0, k, 0), "sw%d" % k, 2.0)
        dma("Y", ext("dn", k * n, k * n + n), cut("FS", 0, k, 1), "sd%d" % k, 2.0)
    byname, bytile = {}, {}
    for i, o in enumerate(ops):
        deps = set()
        names = set(r[0] for r in o["R"] + o["W"])
        for j in set(j for nm in names for j in byname.get(nm, [])):
            p = ops[j]
            if hits(o["R"], p["W"]) or hits(o["W"], p["W"]) or hits(o["W"], p["R"]):
                deps.add(j)
        for tl in o["P"]:
            for j in bytile.get(tl, []):
                p = ops[j]
                if len(p["ways"]) > 1 or list(p["ways"]) != list(o["ways"]) or tl in p["PW"] or tl in o["PW"]:
                    deps.add(j)
            bytile.setdefault(tl, []).append(i)
        for nm in names:
            byname.setdefault(nm, []).append(i)
        o["deps0"] = deps
        o["only"] = list(o["ways"])[0]
    return ops, bytile


def hits(x, y):
    return any(a[0] == b[0] and a[1] < b[2] and b[1] < a[2] for a in x for b in y)


def schedule(ops, bytile, win, stag, lift, vpen):
    N_ = len(ops)
    succ = [[] for _ in ops]
    for i, o in enumerate(ops):
        o["deps"] = set(o["deps0"])
        o["inc"] = False
        for j in o["deps"]:
            succ[j].append(i)
    rank = [0.0] * N_
    for i in range(N_ - 1, -1, -1):
        rank[i] = min(w[1] for w in ops[i]["ways"].values()) + ops[i]["lat"] + max([LAT + rank[j] for j in succ[i]] + [0.0])
        rank[i] += 100.0 * ops[i].get("first", 0)
    prio = [rank[i] - stag * (ops[i]["tag"] or 0) + lift[i] for i in range(N_)]
    free = {e: 0.0 for e in "VSPGY"}
    end, order, at = {}, [], {}
    left = [len(o["deps"]) for o in ops]
    ready = [i for i in range(N_) if left[i] == 0]
    for i in ready:
        at[i] = 0.0
    bank, holder, togo = {}, [None] * 8, {tl: len(v) for tl, v in bytile.items()}
    while ready:
        cand = [(max([end[j] for j in bytile[holder[b_]]]) + LAT if holder[b_] is not None else 0.0, b_)
                for b_ in range(8) if holder[b_] is None or togo[holder[b_]] == 0]
        opts = []
        for i in ready:
            o = ops[i]
            st, pick = at[i], None
            new = [tl for tl in o["P"] if tl not in bank]
            if new:
                if len(cand) < (2 if "P" in o["ways"] else 1):
                    continue
                pick = min(cand)
                st = max(st, pick[0])
            if len(o["ways"]) == 1:
                e = o["only"]
            else:
                e = "V" if max(st, free["V"]) + o["ways"]["V"][1] + vpen[i] < max(st, free["S"]) + o["ways"]["S"][1] else "S"
            opts.append((max(st, free[e]), i, e, pick, new))
        if not opts:
            return None, None, 1e9
        t0 = min(x[0] for x in opts)
        st, i, e, pick, new = max((x for x in opts if x[0] <= t0 + win), key=lambda x: prio[x[1]])
        o = ops[i]
        if new:
            if holder[pick[1]] is not None:
                o["deps"] |= set(bytile[holder[pick[1]]])
            holder[pick[1]] = new[0]
            bank[new[0]] = pick[1]
        for tl in o["P"]:
            togo[tl] -= 1
        o["eng"], o["calls"], o["cost"], o["start"] = e, o["ways"][e][0], o["ways"][e][1], st
        free[e] = st + o["cost"]
        end[i] = st + o["cost"] + o["lat"]
        order.append(i)
        ready.remove(i)
        for j in succ[i]:
            left[j] -= 1
            if left[j] == 0:
                ready.append(j)
                at[j] = max(end[x] for x in ops[j]["deps0"]) + LAT
    return order, bank, max(end.values())


def plan(win, stag, pen, rounds, seed):
    ops, bytile = build()
    rng = np.random.default_rng(seed)
    N_ = len(ops)
    lift, vpen = [0.0] * N_, [pen] * N_
    both = [i for i in range(N_) if len(ops[i]["ways"]) > 1 and ops[i]["ways"]["S"][1] > 0.3]
    best = schedule(ops, bytile, win, stag, lift, vpen)[2]
    for _ in range(rounds):
        l2, v2 = list(lift), list(vpen)
        kind = int(rng.integers(0, 3))
        if kind == 0:
            lo, up = int(rng.integers(0, N_)), float(rng.normal()) * 3.0
            for i in range(lo, min(N_, lo + int(rng.integers(1, 30)))):
                l2[i] += up
        elif kind == 1:
            for i in rng.integers(0, N_, 8):
                l2[int(i)] += float(rng.normal()) * 2.0
        else:
            for i in rng.integers(0, len(both), 2):
                v2[both[int(i)]] = float(rng.choice([-1.0, 0.0, 0.5, 1.5, 9.0]))
        got = schedule(ops, bytile, win, stag, l2, v2)[2]
        if got <= best:
            best, lift, vpen = got, l2, v2
    order, bank, total = schedule(ops, bytile, win, stag, lift, vpen)
    pos = {i: x for x, i in enumerate(order)}
    last = {}
    for i in order:
        o = ops[i]
        need = {}
        for j in o["deps"]:
            p = ops[j]
            if p["sem"] is None:
                if p["eng"] == "P" and o["eng"] == "P":
                    continue
                if p["eng"] not in need or pos[j] > pos[need[p["eng"]]]:
                    need[p["eng"]] = j
            elif hits(o["R"] + o["W"], p["W"]) or p["calls"][0][0] != "send":
                need[p["sem"]] = j
            else:
                need["left_" + p["sem"]] = j
        o["need"] = []
        for key, j in sorted(need.items()):
            if pos[j] > last.get((o["eng"], key), -1):
                last[(o["eng"], key)] = pos[j]
                o["need"].append((j, key if key.startswith("left_") else None))
                ops[j]["inc"] = True
    cnt = {}
    for i in order:
        o = ops[i]
        if o["sem"] is None and o["inc"]:
            cnt[o["eng"]] = cnt.get(o["eng"], 0) + 1
            o["sig"] = ("s" + o["eng"], cnt[o["eng"]])
        elif o["sem"] is not None:
            o["sig"] = (o["sem"], o["val"])
    return ops, order, bank, total


PLAN = plan(0.08, 1.0, 0.8, 1800, 0)


def helpers(topo, src, dst):
    c = [x for x in topo.cores_of(src) if x != src and topo.may_write(x, dst)]
    return [x for x in c if topo.die(x) == topo.die(src)] + [x for x in c if topo.die(x) != topo.die(src)]


def route(T, topo, r, kind, which):
    src = T.cores[r]
    dst = T.cores[(r + kind) % NR]
    return dst, (dst if topo.may_write(src, dst) else helpers(topo, src, dst)[which])


def rank_program(g, core, T, topo):
    ops, order, bank, _ = PLAN

    def res(ap):
        if not isinstance(ap, tuple):
            return ap
        if ap[0] == "i":
            return res(ap[1]).indirect(res(ap[2]))
        if ap[0] == "p":
            return T["pb%d" % bank[ap[1]]][(slice(None),) + ap[2]]
        if ap[1] in HOME:
            pool, at = HOME[ap[1]]
            lo, hi, st = ap[2][0].indices(BUF[ap[1]][1][1])
            return T[pool][:, at + lo:at + hi:st] if st != 1 else T[pool][:, at + lo:at + hi]
        return T[ap[1].replace("wsx", "wsg")][(slice(None),) + tuple(slice(x.start, x.stop) if isinstance(x, slice) and x.step == 1 else x for x in ap[2])]

    left = []

    def write(parts, sem, high):
        (to, d_, s_, ne), = parts
        eng = topo.engines(core, to)
        eng = eng[::-1] if high else eng
        rid, pid = topo.addr(to, core)
        own = "left_" + sem in SEMAPHORES
        g.remote_dma(res(d_), res(s_), T.sem[sem], T.sem["left_" + sem if own else "sent"], pid, rid, sum(1 << e for e in eng[:ne]))
        if own:
            left.append(("left_" + sem, ne))
        return 0 if own else ne

    rank = T.rank_of(core)
    sent = 0
    if rank is None:
        for i in order:
            name, args, kw = ops[i]["calls"][0]
            if name != "send":
                continue
            for r in range(NR):
                mine = [(route(T, topo, r, args[0], p[3])[0], p[0], p[0], p[2]) for p in args[1] if route(T, topo, r, args[0], p[3])[1] == core]
                if mine:
                    g.wait_ge(T.sem[args[2]], sum(p[3] for p in mine))
                    sent += write(mine, args[2], False)
        for s_, v in left + ([("sent", sent)] if sent else []):
            g.wait_ge(T.sem[s_], v)
        return
    Q = {"V": g.vector, "S": g.scalar, "P": g.tensor, "G": g, "Y": g.sync}
    call = {
        "tensor_scalar": g.vector.tensor_scalar, "tensor_tensor": g.vector.tensor_tensor, "tensor_copy": g.vector.tensor_copy,
        "memset": g.vector.memset, "tensor_tensor_scan": g.vector.tensor_tensor_scan, "activation": g.scalar.activation,
        "matmul": g.tensor.matmul, "iota": g.iota}
    tail = []
    for i in order:
        o = ops[i]
        q = Q[o["eng"]]
        for j, key in o["need"]:
            q.wait_ge(T.sem[key or ops[j]["sig"][0]], ops[j]["sig"][1])
        ins = None
        for name, args, kw in o["calls"]:
            if name == "send":
                sent += write([(route(T, topo, rank, args[0], p[3])[1], p[0], p[1], p[2]) for p in args[1]], args[2], args[3])
            elif name == "dma_start":
                q.dma_start(res(args[0]), res(args[1])).then_inc(T.sem[o["sem"]], 16)
                if not o["inc"]:
                    tail.append(o["sem"])
            else:
                ins = call[name](*[res(x) for x in args], **kw)
        if ins is not None and o["inc"]:
            ins.then_inc(T.sem[o["sig"][0]], 1)
    for s_, v in left + [("sent", sent)] + [(s_, 16) for s_ in tail]:
        g.wait_ge(T.sem[s_], v)
